import numpy as np, ml_dtypes
CORES = [24,25,26,27,28,29,30,31]
N = 8
import mx_ref
BF = ml_dtypes.bfloat16
def gcols(t, e):
    v = np.concatenate([t.reshape(8, 16, -1, 4), np.zeros((8, 16, 1, 4), BF)], axis=2)
    return np.ascontiguousarray(np.stack([v[g][:, e[g]] for g in range(8)])).reshape(128, -1)
def tile(rs):
    return np.stack(rs, axis=2).reshape(128, -1).astype(BF)
def pick(q, e):
    c = np.concatenate([q[0].reshape(128, -1, 4), np.zeros((128, 1, 4), np.uint8)], axis=1); s = np.concatenate([q[1], np.ones((16, 1), np.uint8)], axis=1)
    return (np.ascontiguousarray(c[:, e].reshape(128, -1)), np.ascontiguousarray(s[:, e]))
def join(*qs):
    return (np.concatenate([q[0] for q in qs], axis=1), np.concatenate([q[1] for q in qs], axis=1))
def put(q, e, v):
    c, s = q[0].reshape(128, -1, 4).copy(), q[1].copy(); c[:, e] = v[0].reshape(128, -1, 4); s[:, e] = v[1]
    return (c.reshape(128, -1), s)
def pk(c, s):
    return (np.ascontiguousarray(c), mx_ref.live(s))
def emit(q):
    return q[0], q[1]
def packed(v, rng):
    q = [mx_ref.quantize(np.ascontiguousarray(v[r])) for r in range(N)]
    return np.stack([a for a, b in q]), np.stack([mx_ref.plane(b, rng) for a, b in q])
def values_of_codes():
    e, c = np.zeros((128, 128, 4), np.float32), np.zeros((128, 2, 4), np.uint8)
    e[np.arange(128), np.arange(128), 0] = 1
    c[:127, :, 0] = np.arange(256).reshape(2, 128).T[:127]
    return mx_ref.matmul(mx_ref.quantize(e.reshape(128, 512).astype(BF)), (c.reshape(128, 8), np.full((16, 2), 127, np.uint8))).T.reshape(-1).astype(np.float64)
CODE_VALUE, SCALE_VALUE = values_of_codes(), 2.0 ** (np.arange(256) - 127.0)
def decode(q):
    return (CODE_VALUE[q[0]].reshape(16, 8, -1, 4) * SCALE_VALUE[q[1]][:, None, :, None] + 0.0).reshape(128, -1).astype(np.float32)
def f(rng, *shape):
    return mx_ref.flush((rng.standard_normal(shape, dtype=np.float32) * np.exp2(rng.integers(-2, 3, shape[:-1] + (1,)))).astype(BF))
def wide(rng, *shape, cols=0):
    v = rng.standard_normal(shape, dtype=np.float32) * np.exp2(rng.integers(-12, 13, shape)).astype(np.float32)
    if cols: v *= np.repeat(np.exp2(rng.integers(-cols, cols + 1, shape[:-2] + (1, shape[-1] // 4))) * (rng.random(shape[:-2] + (1, shape[-1] // 4)) > 0.0625), 4, axis=-1).astype(np.float32)
    return mx_ref.flush(v.astype(BF))
C, H = 512, 256
def order(p):
    return np.argsort(p[::16] + np.float32(0.0), axis=1, kind="stable")
def places(e):
    at = np.full((8, C + H), -1)
    np.put_along_axis(at, e, np.tile(np.arange(C), (8, 1)), axis=1)
    return at
def mean(a, b):
    return ((a.astype(np.float32) + b.astype(np.float32)) * np.float32(0.5)).astype(BF)
def layer(w, q):
    return tile([mx_ref.matmul(pick(w, np.arange(128 * b, 128 * b + 128)), q) * np.float32(0.03125) for b in range(4)])
def big(v, k=1):
    v = v.astype(np.float32) * np.float32(k)
    v[np.abs(v) < np.float32(2.0 ** -16)] = 0
    return v.astype(BF)
def numbers_of(rng):
    return {"x": big(f(rng, N, 128, 4 * C)), "u": np.array(f(rng, N, 128, 512)), "v": np.array(f(rng, N, 128, 512))}
def weights(rng, w):
    c, p = packed(w, rng)
    return {"wc": c, "ws": p}
def still(rng):
    w = np.zeros((N, 128, 4, 128, 4), np.float32)
    i = np.arange(128)
    for b in range(4): w[:, i, b, i, b] = 32
    return weights(rng, w.reshape(N, 128, 2048).astype(BF))
def signs(rng):
    g = rng.permutation(8)
    return ((g[None, :] + np.arange(N)[:, None]) % 4 < 2) * 2.0 - 1.0
def setup_inputs(rng):
    return {**numbers_of(rng), **weights(rng, f(rng, N, 128, 2048))}
def setup_inputs_ties(rng):
    d = numbers_of(rng)
    e = rng.permutation(N)
    x = d["x"].reshape(N, 8, 16, C, 4)
    for r in range(N):
        k = np.zeros(C, int) if r == e[0] else rng.permutation(C) % 3
        a = x[r][:, :8, :3].copy()
        a[:, :, 2] = 0
        x[r][:, :8] = a[:, :, k]
    u = d["u"].reshape(N, 8, 16, 128, 4)
    u[:, :, 8:, ::16] = 0
    w = np.array(f(rng, N, 128, 2048)).reshape(N, 8, 16, 4, 8, 16, 4)
    w[:, :, 8:, :, :, :8] = 0
    return {"x": x.reshape(N, 128, 4 * C), "u": u.reshape(N, 128, 512), "v": d["v"], **weights(rng, w.reshape(N, 128, 2048))}
def setup_inputs_near(rng):
    d = numbers_of(rng)
    x = d["x"].astype(np.float32).reshape(N, 8, 16, C, 4)
    s = (C - 1 - np.arange(C)) // 3
    g = ((s[:, None] >> np.arange(8)) & 1) * np.exp2(np.arange(8) - 23.0)
    sign = signs(rng)
    x[:, :, 0] = 0
    x[:, :, 0, :, 0] = sign[:, :, None]
    x[:, :, 8] = g[:, :4]
    x[:, :, 9] = g[:, 4:]
    x[:, :, 10:] = rng.integers(4, 8, (N, 8, 6, C, 4)) * rng.choice([-1.0, 1.0], (N, 8, 6, C, 4)) * 2.0 ** -20
    u = d["u"].reshape(N, 128, 128, 4)
    small = rng.permutation(N) < N // 2
    one = np.where(small, 0.0, 1.0).astype(np.float32).astype(BF)
    k = np.where(small[:, None], sign * 2.0 ** -30, 1.0).astype(np.float32).astype(BF)
    u[:, :, ::16] = 0
    for i in range(8):
        u[:, 16 * i, 16 * i, 0] = one
        u[:, 16 * i + 8:16 * i + 10, 16 * i] = k[:, i][:, None, None]
    return {"x": x.reshape(N, 128, 4 * C).astype(BF), "u": u.reshape(N, 128, 512), "v": d["v"], **still(rng)}
def setup_inputs_huge(rng):
    d = numbers_of(rng)
    x = 2.0 ** 30 * (0.6 + 0.4 * rng.random((N, 128, C, 4)))
    c = np.stack([rng.permutation(C) % 2 * 2.0 - 1.0 for r in range(N)])
    c[(np.arange(N) + rng.integers(N)) % N < N // 2] = 1
    x *= c[:, None, :, None]
    u = d["u"].reshape(N, 128, 128, 4)
    a = 2.0 ** 30 * (1 - 0.25 * rng.random((N, 128, 8, 4))) * signs(rng)[:, None, :, None]
    u[:, :, ::16] = a.astype(np.float32).astype(BF)
    return {"x": x.astype(np.float32).reshape(N, 128, 4 * C).astype(BF), "u": u.reshape(N, 128, 512), "v": d["v"], **still(rng)}
def setup_inputs_sizes(rng):
    d = setup_inputs(rng)
    d["x"] = big(d["x"], np.exp2(rng.permutation(N) * (16 // N))[:, None, None])
    return d
def setup_inputs_spread(rng):
    d = numbers_of(rng)
    d["x"] = big(wide(rng, N, 128, 4 * C, cols=6))
    w = np.array(f(rng, N, 128, 2048)).reshape(N, 128, 4, 8, 16, 4)
    g = rng.integers(0, 8, N)
    for r in range(N): w[r, :, :, g[r]] = 0
    return {**d, **weights(rng, w.reshape(N, 128, 2048))}
def check_inputs(d):
    b = []
    for k in ("x", "u", "v"):
        a = np.abs(d[k].astype(np.float32))
        if not (np.isfinite(a).all() and ((a == 0) | (a >= 2.0 ** -30) & (a <= 2.0 ** 30)).all()): b.append("a value of " + k)
    if ((d["wc"] == 0x7F) | (d["wc"] == 0xFF)).any(): b.append("a code of wc")
    least, most = [int(mx_ref.quantize(np.full((128, 16), k, np.float32).astype(BF))[1][0, 0]) for k in (2.0 ** -30, 2.0 ** 30)]
    for p in d["ws"]:
        s = mx_ref.live(p)
        if ((s != 1) & ((s < least) | (s > most))).any(): b.append("a scale of ws")
    return b
def reference(x, u, v, wc, ws):
    qu = [mx_ref.quantize(u[r]) for r in range(N)]
    lay = [pk(wc[r], ws[r]) for r in range(N)]
    own, score, lists = [], [], []
    for r in range(N):
        q = mx_ref.quantize(x[r])
        own.append(decode(q).astype(BF))
        score.append(mx_ref.matmul(qu[r], q))
        lists.append([order(score[r])])
    held = [own[r] for r in range(N)]
    for t in range(2):
        pairs = []
        for r in range(N):
            e = lists[r][t]
            pairs.append(mx_ref.quantize(mean(gcols(held[r], e[:, ::2]), gcols(held[r], e[:, 1::2]))))
        for r in range(N):
            q = mx_ref.quantize(layer(lay[r], pairs[(r - 1) % N]))
            held[r] = np.concatenate([own[r], decode(q).astype(BF)], axis=1)
            lists[r].append(order(np.concatenate([score[r], mx_ref.matmul(qu[r], q)], axis=1))[:, :C])
    half = np.tile(np.arange(C) // 2, (8, 1))
    value, used = [], []
    for r in range(N):
        first = layer(lay[r], mx_ref.quantize(gcols(held[r], lists[r][2][:, :H])))
        value.append(np.concatenate([first, np.zeros((128, 4 * (C - H)), BF)], axis=1))
        used.append(np.tile((np.arange(C) < H).astype(np.int64), (8, 1)))
    now = [own[r] for r in range(N)]
    count = [np.zeros((8, C), np.int64) for r in range(N)]
    for t in (2, 1, 0):
        back, flag = [], []
        for r in range(N):
            at = places(lists[r][t])
            is_used = np.take_along_axis(np.concatenate([used[r], np.zeros((8, 1), np.int64)], axis=1), at, axis=1)
            now[r] = mean(now[r], gcols(value[r], at[:, :C]))
            count[r] = count[r] + is_used[:, :C]
            if t > 0:
                back.append(mx_ref.quantize(gcols(value[r], at[:, C:])))
                flag.append(is_used[:, C:])
        if t > 0:
            for r in range(N):
                e = (r + 1) % N
                value[r] = gcols(decode(back[e]).astype(BF), half)
                used[r] = np.take_along_axis(flag[e], half, axis=1)
    y, uc = np.zeros((N, 128, C), np.float32), np.zeros((N, 8, C), np.float32)
    oc, osc = np.zeros((N, 128, 4 * C), np.uint8), np.zeros((N, 16, C), np.uint8)
    for r in range(N):
        q = mx_ref.quantize(now[r])
        y[r] = mx_ref.matmul(mx_ref.quantize(v[r]), q)
        uc[r] = count[r]
        oc[r], osc[r] = emit(q)
    return {"y": y, "uc": uc, "oc": oc, "osc": osc}

@@ -1,0 +1,574 @@
+from concourse.bass import DstId, RemoteDMATransfer
+from concourse.mybir import dt, AluOpType as Op, ActivationFunctionType as Fn
+
+F8, U8, BF, F32, I32, U16, F16 = "float8_e4m3fn_x4", "uint8", "bfloat16", "float32", "int32", "uint16", "float16"
+FAR = 4e29
+LOW = 30000.0
+SCRATCH = {}
+PLACE = {}
+
+
+def _b(dtype, **kw):
+    for k in kw:
+        SCRATCH[k] = ("sbuf", [128, kw[k]], dtype)
+        PLACE[k] = (k, 0, kw[k])
+
+
+def _pack(buf, dtype, **kw):
+    at = 0
+    for k in kw:
+        PLACE[k] = (buf, at, kw[k])
+        at += kw[k]
+    SCRATCH[buf] = ("sbuf", [128, at], dtype)
+
+
+def _same(buf, **kw):
+    for k in kw:
+        PLACE[k] = (buf, 0, kw[k])
+
+
+def _mx(**kw):
+    for k in kw:
+        _b(F8, **{"q" + k: kw[k]})
+        _b(U8, **{"s" + k: kw[k]})
+
+
+EQ = -1
+AHEAD = {0: [24, 20]}
+
+
+def tiles_of(slots, n):
+    out, at = [], 0
+    for k in range(0, len(slots), 4):
+        s = slots[k:k + 4]
+        w = max(128, n if EQ in s else 16 * max(s) + 16)
+        out.append((at, w, s))
+        at += w
+    return out, at
+
+
+OT, OF = tiles_of([EQ] + list(range(31, -1, -1)), 512)
+PT, PF = tiles_of(list(range(15, -1, -1)), 256)
+_b(BF, xt=2048, ut=512, vt=512, ct0=2048, ct1=1536, ones=512, blk=128, grp=128,
+   of=4 * OF, pf=4 * PF, junk=2048, aux=1024, at1=768, ra=272, rb=272, rc=272,
+   th=2048, h=3072, wm=3072, mid=1024, z1=1024, z2=1024, pt=1024, et=1024, v2=1024, d1=1024,
+   v2h=1024, d1q=1088, d0h=1088, x2q=2048, x1h=2048, xo=2048)
+_b(F32, dm=512, dl=512, dm16=16, rst=512, c15=512, zero=512, io=768, io2=512, osr=512, psr=256, qmk=512, osc_=512, psc=256,
+   lst=512, ssr=512, ssc=512, pvs=32, ww=40, pb1=768, pb2=768, ob1=768, ob2=768, at2=768, ucr=512, yo=512)
+_b(F16, rsth=512, lmk=512, lsc=512, mkh=512, sch=512)
+_same("qmk", omk=512, pmk=256, smk=512, pvm=32)
+_same("lmk", omk2=512, pmk2=256)
+_same("lsc", osc2=512, psc2=256)
+_pack("small", F32, c16=32, ors=32, orc=32, rk=32, prs=16, prc=16, pl1=16, pl2=16, cut2=16, u2=32, u1=32, u0=32, ucs=32, uct=32)
+_b(I32, ii=32, jj=32, pj=32)
+_pack("whole", I32, c16i=32, pli=16, plh=16, rki=32, rkh=32)
+_b(U16, ex0=8, pju=32, a1u=16, a2u=16, la1=16, la2n=16, la2m=16)
+_pack("offs", U16, rku=32, rhu=32, lu=32, segu=16, plu1=16, plu2=16, elu1=32, elu2=16, h1u=32, p2u=32, o1u=32,
+      o0u=32, ucu=32)
+_mx(x=512, u=128, ub=128, v=128, w=512, e=512, c=384,
+    z1=256, z2=256, lz1=256, lz2=256, p1=256, p2=256, et=256, v2=256, lv2=256, d1=256, ld1=256, xo=512)
+for _k, _d in (("q", F8), ("s", U8)):
+    _pack(_k + "flags", _d, **{_k + "of": OF, _k + "pf": PF, _k + "seg": 256, _k + "aux": 256})
+for _k in range(8):
+    SCRATCH["ps%d" % _k] = ("psum", [128, 512], F32)
+    PLACE["ps%d" % _k] = ("ps%d" % _k, 0, 512)
+LOADS = ["lx0", "lx1", "ldu", "ldv", "lwc", "lws"]
+ARRIVE = ["rz1", "rz2", "rv2", "rd1", "ra1", "ra2"]
+SEMAPHORES = ["c_t", "c_v", "c_a", "c_g", "sty", "sto", "sent"] + LOADS + ARRIVE
+
+
+def rank_program(g, core, T, topo):
+    rank = T.rank_of(core)
+    if rank is None:
+        return
+    cores = T.cores
+    N = len(cores)
+    nxt, prv, prv2 = cores[(rank + 1) % N], cores[(rank - 1) % N], cores[(rank - 2) % N]
+    queue = {"t": g.tensor, "v": g.vector, "a": g.scalar, "g": g, "s": g.sync}
+    total = {}
+    clock = {q: {} for q in queue}
+    hist = {}
+
+    def clash(a, b):
+        if a[0] >= b[1] or b[0] >= a[1]:
+            return False
+        if a[2] == b[2] and a[2] > 1 and (a[0] - b[0]) % a[2]:
+            return False
+        return True
+
+    def needs(q, rd, wr, acc=False):
+        need = {}
+        for rs, w in ((rd, False), (wr, True)):
+            for r in rs:
+                psum = r[0][:2] == "ps" and r[0][2:].isdigit()
+                for (ev, eq, reg, ew) in hist.get(r[0], ()):
+                    if psum:
+                        if eq == q and ((acc and q == "t") or not (w or ew)):
+                            continue
+                    elif not (w or ew) or not clash(r[1:], reg):
+                        continue
+                    sem, val, snap = ev
+                    if need.get(sem, (0,))[0] < val:
+                        need[sem] = (val, snap)
+        return need
+
+    def do_waits(q, need):
+        have = clock[q]
+        need = {s: v for s, v in need.items() if have.get(s, 0) < v[0]}
+        for s in list(need):
+            others = [o for o in need if o != s and need[o][1].get(s, 0) >= need[s][0]]
+            if any(need[s][1].get(o, 0) < need[o][0] for o in others):
+                del need[s]
+        for s, (val, snap) in need.items():
+            queue[q].wait_ge(T.sem[s], val)
+            for k, v in snap.items():
+                have[k] = max(have.get(k, 0), v)
+            have[s] = max(have.get(s, 0), val)
+
+    def record(q, ev, rd, wr):
+        for rs, w in ((rd, False), (wr, True)):
+            for r in rs:
+                l = hist.setdefault(r[0], [])
+                if w and r[3] == 1:
+                    l[:] = [e for e in l if not (r[1] <= e[2][0] and e[2][1] <= r[2])]
+                l.append((ev, q, r[1:], w))
+
+    def op(q, fn, rd, wr, acc=False):
+        do_waits(q, needs(q, rd, wr, acc))
+        s = "c_" + q
+        total[s] = total.get(s, 0) + 1
+        fn().then_inc(T.sem[s], 1)
+        snap = dict(clock[q])
+        snap[s] = total[s]
+        record(q, (s, total[s], snap), rd, wr)
+
+    def dma(q, fn, rd, wr, sem):
+        do_waits(q, needs(q, rd, wr))
+        total[sem] = total.get(sem, 0) + 16
+        fn().then_inc(T.sem[sem], 16)
+        record(q, (sem, total[sem], dict(clock[q])), rd, wr)
+
+    def width(name):
+        return PLACE[name][2]
+
+    def R(name, lo=0, hi=None, st=1):
+        buf, at, n = PLACE[name]
+        return (buf, at + lo, at + (n if hi is None else hi), st)
+
+    def ap(r):
+        return T[r[0]][:, r[1]:r[2]] if r[3] == 1 else T[r[0]][:, r[1]:r[2]:r[3]]
+
+    def by(r, off):
+        return ap(r).indirect(ap(off))
+
+    def memset(out, c):
+        op("v", lambda: g.vector.memset(ap(out), c), [], [out])
+
+    def copy(out, i, off=None):
+        op("v", lambda: g.vector.tensor_copy(ap(out), by(i, off) if off else ap(i)), [i] + ([off] if off else []), [out])
+
+    def scatter(win, off, i):
+        op("v", lambda: g.vector.tensor_copy(by(win, off), ap(i)), [i, off], [win])
+
+    def tt(out, a, b, o, off=None):
+        op("v", lambda: g.vector.tensor_tensor(ap(out), by(a, off) if off else ap(a), ap(b), o),
+           [a, b] + ([off] if off else []), [out])
+
+    def ts(out, a, s1, o, off=None):
+        col = isinstance(s1, tuple)
+        op("v", lambda: g.vector.tensor_scalar(ap(out), by(a, off) if off else ap(a), ap(s1) if col else s1, None, o),
+           [a] + ([off] if off else []) + ([s1] if col else []), [out])
+
+    def ts2(out, a, s1, o1, s2, o2):
+        op("v", lambda: g.vector.tensor_scalar(ap(out), ap(a), s1, s2, o1, o2), [a], [out])
+
+    def scan(out, a, b, init, o0, o1):
+        op("v", lambda: g.vector.tensor_tensor_scan(ap(out), ap(a), ap(b), init, o0, o1), [a, b], [out])
+
+    def act(out, i, scale=1.0, off=None, accum=None, fn=Fn.Copy, bias=None):
+        col = isinstance(bias, tuple)
+
+        def f():
+            kw = {}
+            if scale != 1.0:
+                kw["scale"] = scale
+            if bias is not None:
+                kw["bias"] = ap(bias) if col else bias
+            if accum:
+                kw["accum_out"] = ap(accum)
+            return g.scalar.activation(ap(out), by(i, off) if off else ap(i), fn, **kw)
+        op("a", f, [i] + ([off] if off else []) + ([bias] if col else []), [out] + ([accum] if accum else []))
+
+    def quant(name, tile, c0=0, n=None):
+        n = width("q" + name) if n is None else n
+        q, s, t = R("q" + name, c0, c0 + n), R("s" + name, c0, c0 + n), R(tile, 4 * c0, 4 * (c0 + n))
+        op("v", lambda: g.vector.quantize_mx(ap(q), ap(s), ap(t)), [t], [q, s])
+
+    def mm(bank, n, sta, c0, mov, m0=0, start=True, stop=True):
+        o = R("ps%d" % bank, 0, n)
+        a, b = R("q" + sta, c0, c0 + 128), R("s" + sta, c0, c0 + 128)
+        c, d = R("q" + mov, m0, m0 + n), R("s" + mov, m0, m0 + n)
+        op("t", lambda: g.tensor.matmul_mx(ap(o), ap(a), ap(b), ap(c), ap(d), start, stop), [a, b, c, d], [o], acc=not start)
+
+    def ps(k, n):
+        return R("ps%d" % k, 0, n)
+
+    def wrap(n, mk, sc, src=None, src2=None, win=None, off=None, score=False):
+        dm, rst = ("dm", "rst") if score else ("dl", "rsth")
+        if win:
+            tt(R(mk, 0, n), win, R(dm, 0, n), Op.add, off=off)
+        elif src2:
+            tt(R(mk, 0, n // 2), src, R(dm, 0, n // 2), Op.add)
+            tt(R(mk, n // 2, n), src2, R(dm, 0, n // 2), Op.add)
+        else:
+            tt(R(mk, 0, n), src, R(dm, 0, n), Op.add)
+        scan(R(sc, 0, n), R(rst, 0, n), R(mk, 0, n), -FAR, Op.min, Op.max)
+
+    def wrapped(sc, n):
+        return R(sc, 15, n, 16)
+
+    def engines(dst, a, b):
+        m = 0
+        for e in topo.engines(core, dst)[a:b]:
+            m |= 1 << e
+        return m
+
+    def send_mx(src, land, dst, sem):
+        rid, pid, _ = topo.addr(dst)
+        ne = len(topo.engines(core, dst))
+        q, s, lq, ls = R("q" + src), R("s" + src), R("q" + land), R("s" + land)
+        do_waits("g", needs("g", [q, s], []))
+        g.remote_dma(out_ap=ap(lq).bitcast(dt.uint8), in_ap=ap(q).bitcast(dt.uint8), remote_sem=T.sem[sem],
+                     local_sem=T.sem.sent, pid=pid, routing_id=rid, dma_engine_mask=engines(dst, 0, ne))
+        g.remote_dma(out_ap=ap(ls), in_ap=ap(s), remote_sem=T.sem[sem],
+                     local_sem=T.sem.sent, pid=pid, routing_id=rid, dma_engine_mask=engines(dst, 0, ne))
+        total["sent"] = total.get("sent", 0) + 2 * ne
+        total[sem] = 2 * ne
+        for r in (lq, ls):
+            hist.setdefault(r[0], []).append(((sem, 2 * ne, {}), "r", r[1:], True))
+
+    def send_list(src, pairs, sem):
+        do_waits("g", needs("g", [R(src)], []))
+        ids = []
+        for land, dst in pairs:
+            rid, pid, _ = topo.addr(dst)
+            ids.append(DstId(rid=rid, pnc=pid))
+        m = engines(pairs[0][1], 8, 12)
+        g.remote_dma_fused([RemoteDMATransfer(dst_ids=ids, dma_engine_mask=m, remote_sem=T.sem[sem], srcs=[T[src][:, :]],
+                                              dsts=[T[land][:, :] for land, dst in pairs])], local_sem=T.sem.sent)
+        total["sent"] = total.get("sent", 0) + 4
+        total[sem] = 4 * len(pairs)
+        for land, dst in pairs:
+            hist.setdefault(land, []).append(((sem, total[sem], {}), "r", R(land)[1:], True))
+
+    def load(q, out, src, sem, code=False):
+        dma(q, lambda: queue[q].dma_start(ap(out).bitcast(dt.uint8) if code else ap(out), src), [], [out], sem)
+    load("s", R("xt", 0, 1024), T.x[:, 0:1024], "lx0")
+    load("a", R("ut"), T.u[:, :], "ldu")
+    load("a", R("xt", 1024, 2048), T.x[:, 1024:2048], "lx1")
+    load("s", R("qw"), T.wc[:, :], "lwc", code=True)
+    load("s", R("sw"), T.ws[:, :], "lws")
+    load("s", R("vt"), T.v[:, :], "ldv")
+
+    def iota(out, pattern, base, cm):
+        if SCRATCH[out[0]][2] == I32:
+            op("g", lambda: g.iota(ap(out), pattern, base, cm), [], [out])
+        else:
+            op("g", lambda: g.iota(ap(out), pattern, base, cm, allow_small_or_imprecise_dtypes=True), [], [out])
+
+    def choose(out, i, pattern, cmp, base, cm):
+        op("g", lambda: g.affine_select(ap(out), ap(i), pattern, cmp, 0.0, base, cm), [i], [out])
+
+    def fill(out, c):
+        iota(out, [[0, len(range(*out[1:]))]], c, 0)
+
+    def pads(name, tiles):
+        for at, w, s in tiles:
+            lo = 16 * min(m for m in s if m != EQ) + 16 if len(s) == 4 else 0
+            yield R(name, 4 * (at + lo), 4 * (at + w))
+
+    memset(R("ones"), 1.0)
+    iota(R("c16i"), [[16, 32]], 0, 0)
+    iota(R("ii"), [[1, 32]], 128, -1)
+    iota(R("pj"), [[0, 32]], 0, 1)
+    iota(R("c15"), [[0, 32], [1, 16]], 0, 0)
+    choose(R("blk"), R("ones", 0, 128), [[-16, 8], [0, 16]], Op.is_ge, 0, 1)
+    choose(R("grp"), R("blk"), [[16, 8], [0, 16]], Op.is_ge, 15, -1)
+    for b in range(4):
+        choose(R("ct0", 512 * b, 512 * b + 512), R("ones"), [[-1, 512]], Op.is_equal, b, 4)
+    for r in pads("of", OT[3:]):
+        fill(r, 0)
+    iota(R("io"), [[1, 768]], 0, 0)
+    for r in pads("pf", PT):
+        fill(r, 0)
+    fill(R("aux"), 0)
+    fill(R("zero"), 0)
+    fill(R("pb1"), 1)
+
+    ts(R("jj"), R("ii"), 15, Op.bitwise_and)
+    ts2(R("dm16"), R("jj", 0, 16), 0.0, Op.is_gt, -FAR, Op.mult)
+    ts(R("ii"), R("pj"), 15, Op.bitwise_and)
+    copy(R("pju"), R("ii"))
+    copy(R("ex0"), R("c16i", 0, 8))
+    act(R("dm"), R("dm16"), off=R("pju"))
+    act(R("rst"), R("c15"), fn=Fn.Sign)
+    act(R("rst"), R("rst"), scale=2 * FAR, bias=-FAR, fn=Fn.Identity)
+    for t in range(4):
+        act(R("ct1", t, 512, 4), R("grp"))
+    for t, k in ((0, 1.0), (1, 1.0), (2, 16.0), (3, 16.0)):
+        act(R("ct1", 512 + t, 1024, 4), R("grp"), scale=k)
+    for t, k in ((0, 0.0), (1, 0.0), (2, 1.0), (3, 1.0)):
+        act(R("ct1", 1024 + t, 1536, 4), R("grp"), scale=k)
+    for r in pads("of", OT[:3]):
+        memset(r, 0.0)
+    ts(R("c16"), R("c16i"), -1.0, Op.add)
+    memset(R("ors"), 0.0)
+    memset(R("prs"), 0.0)
+    quant("u", "ut")
+    op("v", lambda: g.vector.tensor_copy(T.qub[:, 0:128].bitcast(dt.uint32), T.qu[:, 0:128].bitcast(dt.uint32).indirect(T.ex0[:, 0:8])),
+       [R("qu"), R("ex0")], [R("qub")])
+    copy(R("sub"), R("su"), R("ex0"))
+    quant("x", "xt", 0, 256)
+    quant("x", "xt", 256, 256)
+    ts2(R("rsth"), R("c15"), 0.0, Op.is_gt, 2 * LOW, Op.mult)
+
+    SC = {"o": "osc_", "p": "psc"}
+
+    def sort_begin(n, p, q, meanwhile=None):
+        mm(0, n, "ub", 0, q)
+        mm(1, n, "ub", 0, q)
+        if meanwhile:
+            meanwhile()
+        wrap(n, p + "mk", SC[p], src=ps(0, n), score=True)
+
+    def scalar_of(p, m):
+        return R(SC[p], 16 * m + 15, 16 * m + 16)
+
+    def compare(p, at, t, m):
+        f = p + "f"
+        ts(R(f, 4 * at + t, 4 * (at + 16 * m + 16), 4), ps(0, 16 * m + 16), scalar_of(p, m), Op.is_gt)
+        if m:
+            act(R("junk", 512 * t, 512 * t + 16 * m), R(f, 4 * at + t, 4 * (at + 16 * m), 4), accum=R(p + "rs", m, m + 1))
+
+    def compare_scalar(p, at, t, m):
+        f, k = p + "f", 512 * t
+        act(R("junk", k, k + 16 * m + 16), ps(1, 16 * m + 16), fn=Fn.Sign, scale=-1.0, bias=scalar_of(p, m))
+        act(R(f, 4 * at + t, 4 * (at + 16 * m), 4), R("junk", k, k + 16 * m), fn=Fn.Relu, scale=-1.0, accum=R(p + "rs", m, m + 1))
+        act(R(f, 4 * (at + 16 * m) + t, 4 * (at + 16 * m + 16), 4), R("junk", k + 16 * m, k + 16 * m + 16), fn=Fn.Relu, scale=-1.0)
+
+    def equal(out, n, p):
+        tt(out, R(SC[p], 0, n), ps(0, n), Op.is_equal)
+
+    def summed(p, tile, first=False, last=False):
+        at, w, s = tile
+        f = p + "f"
+        quant(f, f, at, w)
+        mm(2, w, "c", 0, f, m0=at, start=first, stop=last)
+
+    def sort_end(n, p, rk, u16):
+        tt(R(p + "rc"), R("c16", 0, n // 16), R(p + "rs"), Op.subtract)
+        wrap(n, p + "mk2", p + "sc2", src=ps(2, n))
+        tt(R(rk), wrapped(p + "sc2", n), R(p + "rc"), Op.add)
+        copy(R(u16), R(rk))
+
+    sort_begin(512, "o", "x")
+    ahead = [m for ms in AHEAD.values() for m in ms]
+    for k, tile in enumerate(OT):
+        at, w, s = tile
+        for t, m in enumerate(s):
+            if m != EQ and m not in ahead:
+                compare("o", at, t, m)
+        if EQ in s:
+            equal(R("of", 4 * at + s.index(EQ), 4 * (at + 512), 4), 512, "o")
+        for m in AHEAD.get(k, ()):
+            l = [i for i, o in enumerate(OT) if m in o[2]][0]
+            compare_scalar("o", OT[l][0], OT[l][2].index(m), m)
+        if k == 0:
+            quant("c", "ct1")
+        if k == 4:
+            act(R("dl"), R("dm"), scale=LOW / FAR)
+        summed("o", tile, first=k == 0, last=tile is OT[-1])
+    quant("e", "ct0")
+    for b in range(4):
+        mm(4 + b, 512, "e", 128 * b, "x")
+    for b in range(4):
+        act(R("th", 512 * b, 512 * b + 512), ps(4 + b, 512), scale=0.5)
+    act(R("osr"), ps(1, 512))
+    sort_end(512, "o", "rk", "rku")
+    scatter(R("lst"), R("rku"), R("io", 0, 512))
+    wrap(512, "lmk", "lsc", src=R("lst", 0, 512, 2), src2=R("lst", 1, 512, 2))
+    copy(R("lu"), wrapped("lsc", 512))
+
+    def pair_up(z, win, even, odd, mid):
+        copy(mid(0), win(0), off=even)
+        for t in range(1, 4):
+            act(mid(t), win(t), off=even)
+        for t in range(4):
+            tt(R(z, t, 1024, 4), win(t), mid(t), Op.add, off=odd)
+        quant(z, z)
+
+    pair_up("z1", lambda t: R("th", 512 * t, 512 * t + 512), R("lu", 0, 16), R("lu", 16, 32),
+            lambda t: R("h", 768 * t, 768 * t + 512, 2))
+    send_mx("z1", "lz1", nxt, "rz1")
+
+    for c in range(2):
+        act(R("ssr", c, 512, 2), R("osr"), off=R("lu", 16 * c, 16 * c + 16))
+    wrap(512, "smk", "ssc", src=R("ssr"), score=True)
+    memset(R("ww"), 9e29)
+    copy(R("ww", 0, 32), wrapped("ssc", 512))
+    wrap(32, "pvm", "pvs", src=R("ssr", 15, 512, 16), score=True)
+    for t in range(4):
+        act(R("h", 768 * t + 1, 768 * t + 512, 2), R("th", 512 * t, 512 * t + 512), off=R("lu", 16, 32))
+    iota(R("io2"), [[0, 2], [1, 256]], 0, 0)
+    fill(R("at1"), 256)
+    fill(R("pb2"), 1)
+    iota(R("at2"), [[1, 768]], 0, 0)
+    for b in ("ra", "rb", "rc"):
+        fill(R(b, 256, 272), 256)
+    for b in ("d1q", "d0h"):
+        for t in range(4):
+            fill(R(b, 272 * t + 256, 272 * t + 272), 0)
+
+    def layer(q, tile):
+        for b in range(4):
+            mm(4 + b, 256, "w", 128 * b, q)
+        for b in range(4):
+            if b % 2:
+                ts(R(tile, b, 1024, 4), ps(4 + b, 256), 0.03125, Op.mult)
+            else:
+                act(R(tile, b, 1024, 4), ps(4 + b, 256), scale=0.03125)
+
+    def merge(t, need, first, second):
+        s = str(t)
+        layer("lz" + s, "pt")
+        quant("p" + s, "pt")
+        sort_begin(256, "p", "p" + s, first)
+        act(R("psr"), ps(1, 256))
+        for b in range(4):
+            mm(4 + b, 256, "e", 128 * b, "p" + s)
+        for k, m in enumerate(PT[0][2]):
+            compare_scalar("p", PT[0][0], k, m)
+        for k in range(need // 256):
+            ts(R("aux", 2 + k, 1024, 4), ps(0, 256), R("pvs", 16 * k + 15, 16 * k + 16), Op.is_ge)
+        quant("seg", "aux")
+        mm(3, 256, "c", 256, "seg")
+        for k, m in enumerate(PT[1][2]):
+            compare("p", PT[1][0], k, m)
+        equal(R("aux", 0, 1024, 4), 256, "p")
+        wrap(256, "lmk", "lsc", src=ps(3, 256))
+        copy(R("segu"), wrapped("lsc", 256))
+        tt(R("aux", 1, 1024, 4), R("ww"), R("psr"), Op.is_le, off=R("segu"))
+        quant("aux", "aux")
+        mm(2, 256, "c", 128, "aux", start=True, stop=False)
+        summed("p", PT[1])
+        for tile in PT[2:]:
+            for k, m in enumerate(tile[2]):
+                compare("p", tile[0], k, m)
+            summed("p", tile)
+        summed("p", PT[0], last=True)
+        for b in range(4):
+            act(R("h", 768 * b + 512, 768 * b + 768), ps(4 + b, 256), scale=0.5)
+        second()
+        sort_end(256, "p", "pl" + s, "plu" + s)
+        pb, ob, pl = R("pb" + s), R("ob" + s), R("plu" + s)
+        scatter(pb, pl, R("zero", 0, 256))
+        scan(R("ob" + s, 0, need), R("pb" + s, 0, need), R("zero", 0, need), -1.0, Op.add, Op.add)
+        scatter(ob, pl, R("io", 512, 768))
+
+    held = lambda t: R("h", 768 * t, 768 * t + 768)
+
+    def halved_ranks():
+        copy(R("rki"), R("rk"))
+        ts(R("rkh"), R("rki"), 1, Op.arith_shift_right)
+        copy(R("rhu"), R("rkh"))
+    merge(1, 512, lambda: quant("v", "vt"), halved_ranks)
+    wrap(512, "lmk", "lsc", src=R("ob1", 0, 512, 2), src2=R("ob1", 1, 512, 2))
+    copy(R("elu1"), wrapped("lsc", 512))
+    pair_up("z2", held, R("elu1", 0, 16), R("elu1", 16, 32), lambda t: R("mid", 256 * t, 256 * t + 256))
+    send_mx("z2", "lz2", nxt, "rz2")
+
+    ts(R("pli"), R("pl1"), 512.0, Op.min)
+    ts(R("plh"), R("pli"), 1, Op.arith_shift_right)
+    copy(R("a1u"), R("plh"))
+    send_list("a1u", [("la1", prv)], "ra1")
+    scatter(R("at1"), R("elu1"), R("io2"))
+    fill(R("aux", 3, 1024, 4), 0)
+    for t in range(4):
+        act(R("wm", 768 * t, 768 * t + 512), R("h", 768 * t, 768 * t + 512))
+
+    def mask_places():
+        tt(R("mkh"), R("at1"), R("dl"), Op.add, off=R("rku"))
+
+    def wrap_places():
+        scan(R("sch"), R("rsth"), R("mkh"), -FAR, Op.min, Op.max)
+        copy(R("h1u"), wrapped("sch", 512))
+    merge(2, 256, mask_places, wrap_places)
+    wrap(256, "lmk", "lsc", src=R("ob2", 0, 256))
+    copy(R("elu2"), wrapped("lsc", 256))
+    for t in (1, 0, 3, 2):
+        if t % 2:
+            act(R("et", t, 1024, 4), held(t), scale=2.0, off=R("elu2"))
+        else:
+            ts(R("et", t, 1024, 4), held(t), 2.0, Op.mult, off=R("elu2"))
+    quant("et", "et")
+    ts(R("cut2"), R("pl2"), 256.0, Op.min)
+    copy(R("a2u"), R("cut2"))
+    send_list("a2u", [("la2n", prv), ("la2m", prv2)], "ra2")
+    scatter(R("at2"), R("elu2"), R("io", 512, 768))
+    layer("et", "v2")
+    quant("v2", "v2")
+    send_mx("v2", "lv2", prv, "rv2")
+    for b in range(4):
+        act(R("v2h", 256 * b, 256 * b + 256), ps(4 + b, 256), scale=0.03125 * 0.5)
+    act(R("ra", 0, 256), R("io", 0, 264), off=R("la2n"))
+    act(R("rb", 0, 256), R("io", 0, 264), off=R("la2m"))
+    act(R("rc", 0, 256), R("rb"), off=R("la1"))
+    wrap(512, "lmk", "lsc", win=R("at2"), off=R("rku"))
+    copy(R("p2u"), wrapped("lsc", 512))
+    ts(R("u2"), wrapped("lsc", 512), 512.0, Op.is_ge)
+    for t in range(4):
+        tt(R("wm", 768 * t + 512, 768 * t + 768), held(t), R("v2h", 256 * t, 256 * t + 256), Op.add, off=R("elu2"))
+
+    for b in range(4):
+        mm(4 + b, 256, "e", 128 * b, "lv2")
+    for b in range(4):
+        act(R("d1", b, 1024, 4), ps(4 + b, 256))
+    wrap(512, "lmk", "lsc", win=R("ra"), off=R("h1u"))
+    copy(R("o1u"), wrapped("lsc", 512))
+    ts(R("u1"), wrapped("lsc", 512), 256.0, Op.is_lt)
+    quant("d1", "d1")
+    send_mx("d1", "ld1", prv, "rd1")
+    for b in range(4):
+        act(R("d1q", 272 * b, 272 * b + 256), ps(4 + b, 256), scale=0.25)
+        act(R("x2q", 512 * b, 512 * b + 512), R("wm", 768 * b, 768 * b + 768), scale=0.25, off=R("p2u"))
+    wrap(512, "lmk", "lsc", win=R("rc"), off=R("rhu"))
+    copy(R("o0u"), wrapped("lsc", 512))
+    ts(R("u0"), wrapped("lsc", 512), 256.0, Op.is_lt)
+    for t in range(4):
+        tt(R("x1h", 512 * t, 512 * t + 512), R("d1q", 272 * t, 272 * t + 272), R("x2q", 512 * t, 512 * t + 512), Op.add, off=R("o1u"))
+    tt(R("ucs"), R("u2"), R("u1"), Op.add)
+    tt(R("uct"), R("ucs"), R("u0"), Op.add)
+    copy(R("ucu"), R("uct"))
+    for b in range(4):
+        mm(b, 256, "e", 128 * b, "ld1")
+    for b in range(4):
+        act(R("d0h", 272 * b, 272 * b + 256), ps(b, 256), scale=0.5)
+    act(R("ucr"), R("io", 0, 16), off=R("ucu"))
+    dma("s", lambda: g.sync.dma_start(T.uc[:, :], T.ucr[0:128:16, :]), [R("ucr")], [], "sto")
+    for c, (lo, hi) in enumerate(((0, 352), (352, 512))):
+        for t in range(4):
+            tt(R("xo", 4 * lo + t, 4 * hi, 4), R("d0h", 272 * t, 272 * t + 272), R("x1h", 512 * t + lo, 512 * t + hi), Op.add,
+               off=R("o0u", lo // 16, hi // 16))
+        quant("xo", "xo", lo, hi - lo)
+        q = R("qxo", lo, hi)
+        dma("s", lambda: g.sync.dma_start(T.oc[:, 4 * lo:4 * hi], ap(q).bitcast(dt.uint8)), [q], [], "sto")
+        mm(4 + c, hi - lo, "v", 0, "xo", m0=lo)
+        for k in range(4):
+            e, o, i = ("s", "a")[k // 2], T.osc[4 * k:4 * k + 4, lo:hi], T.sxo[32 * k:32 * k + 4, lo:hi]
+            dma(e, lambda: queue[e].dma_start(o, i), [R("sxo", lo, hi)], [], "sto" if e == "s" else "sty")
+        act(R("yo", lo, hi), ps(4 + c, hi - lo))
+        dma("a", lambda: g.scalar.dma_start(T.y[:, lo:hi], T.yo[:, lo:hi]), [R("yo", lo, hi)], [], "sty")
+
+    for s in SEMAPHORES:
+        if total.get(s, 0):
+            g.wait_ge(T.sem[s], total[s])

@@ -3,7 +3,7 @@ from concourse.mybir import dt, AluOpType as Op, ActivationFunctionType as Fn
 
 F8, U8, BF, F32, I32, U16, F16 = "float8_e4m3fn_x4", "uint8", "bfloat16", "float32", "int32", "uint16", "float16"
 FAR = 4e29
-LOW = 30000.0
+DROP = 1024.0
 SCRATCH = {}
 PLACE = {}
 
@@ -34,7 +34,8 @@ def _mx(**kw):
 
 
 EQ = -1
-AHEAD = {0: [24, 20]}
+AHEAD = {0: [24, 20], 1: [16]}
+LOADED = 9
 
 
 def tiles_of(slots, n):
@@ -52,19 +53,19 @@ PT, PF = tiles_of(list(range(15, -1, -1)), 256)
 _b(BF, xt=2048, ut=512, vt=512, ct0=2048, ct1=1536, ones=512, blk=128, grp=128,
    of=4 * OF, pf=4 * PF, junk=2048, aux=1024, at1=768, ra=272, rb=272, rc=272,
    th=2048, h=3072, wm=3072, mid=1024, z1=1024, z2=1024, pt=1024, et=1024, v2=1024, d1=1024,
-   v2h=1024, d1q=1088, d0h=1088, x2q=2048, x1h=2048, xo=2048)
-_b(F32, dm=512, dl=512, dm16=16, rst=512, c15=512, zero=512, io=768, io2=512, osr=512, psr=256, qmk=512, osc_=512, psc=256,
-   lst=512, ssr=512, ssc=512, pvs=32, ww=40, pb1=768, pb2=768, ob1=768, ob2=768, at2=768, ucr=512, yo=512)
-_b(F16, rsth=512, lmk=512, lsc=512, mkh=512, sch=512)
+   d1q=1088, d0h=1088, x2q=2048, x1h=2048, xo=2048, rst=512, cw=512, gh=512, g1=512, g0=512)
+_b(F32, dm=512, dm16=16, cw16=16, zero=512, io=768, io2=512, osr=512, psr=256, qmk=512, osc_=512, psc=256,
+   lst=512, ssr=512, ssc=512, pvs=32, ww=40, pb1=768, pb2=768, ob1=768, ob2=768, at2=768, ucr=32, yo=512, g2=512)
+_b(F16, lsc=512, sch=512, sc2=512, sc1=512, sc0=512)
 _same("qmk", omk=512, pmk=256, smk=512, pvm=32)
-_same("lmk", omk2=512, pmk2=256)
 _same("lsc", osc2=512, psc2=256)
-_pack("small", F32, c16=32, ors=32, orc=32, rk=32, prs=16, prc=16, pl1=16, pl2=16, cut2=16, u2=32, u1=32, u0=32, ucs=32, uct=32)
+_pack("small", F32, c16=32, ors=32, orc=32, rk=32, prs=16, prc=16, pl1=16, pl2=16, u2=32, u1=32, u0=32, ucs=32, uct=32,
+      cwa=16, cwb=16, up=8)
 _b(I32, ii=32, jj=32, pj=32)
 _pack("whole", I32, c16i=32, pli=16, plh=16, rki=32, rkh=32)
 _b(U16, ex0=8, pju=32, a1u=16, a2u=16, la1=16, la2n=16, la2m=16)
 _pack("offs", U16, rku=32, rhu=32, lu=32, segu=16, plu1=16, plu2=16, elu1=32, elu2=16, h1u=32, p2u=32, o1u=32,
-      o0u=32, ucu=32)
+      o0u=32)
 _mx(x=512, u=128, ub=128, v=128, w=512, e=512, c=384,
     z1=256, z2=256, lz1=256, lz2=256, p1=256, p2=256, et=256, v2=256, lv2=256, d1=256, ld1=256, xo=512)
 for _k, _d in (("q", F8), ("s", U8)):
@@ -180,7 +181,9 @@ def rank_program(g, core, T, topo):
            [a] + ([off] if off else []) + ([s1] if col else []), [out])
 
     def ts2(out, a, s1, o1, s2, o2):
-        op("v", lambda: g.vector.tensor_scalar(ap(out), ap(a), s1, s2, o1, o2), [a], [out])
+        col = isinstance(s1, tuple)
+        op("v", lambda: g.vector.tensor_scalar(ap(out), ap(a), ap(s1) if col else s1, s2, o1, o2),
+           [a] + ([s1] if col else []), [out])
 
     def scan(out, a, b, init, o0, o1):
         op("v", lambda: g.vector.tensor_tensor_scan(ap(out), ap(a), ap(b), init, o0, o1), [a, b], [out])
@@ -213,19 +216,19 @@ def rank_program(g, core, T, topo):
     def ps(k, n):
         return R("ps%d" % k, 0, n)
 
-    def wrap(n, mk, sc, src=None, src2=None, win=None, off=None, score=False):
-        dm, rst = ("dm", "rst") if score else ("dl", "rsth")
-        if win:
-            tt(R(mk, 0, n), win, R(dm, 0, n), Op.add, off=off)
-        elif src2:
-            tt(R(mk, 0, n // 2), src, R(dm, 0, n // 2), Op.add)
-            tt(R(mk, n // 2, n), src2, R(dm, 0, n // 2), Op.add)
-        else:
-            tt(R(mk, 0, n), src, R(dm, 0, n), Op.add)
-        scan(R(sc, 0, n), R(rst, 0, n), R(mk, 0, n), -FAR, Op.min, Op.max)
+    def wrap_scores(mk, sc, lo, hi, src):
+        tt(R(mk, lo, hi), src, R("dm", 0, hi - lo), Op.add)
+        scan(R(sc, lo, hi), R("rst", 0, hi - lo), R(mk, lo, hi), -FAR, Op.min, Op.max)
 
-    def wrapped(sc, n):
-        return R(sc, 15, n, 16)
+    def wrap(sc, lo, hi, src):
+        scan(R(sc, lo, hi), R("cw", 0, hi - lo), src, 0.0, Op.add, Op.min)
+
+    def wrapped(sc, n, lo=0):
+        return R(sc, lo + 15, n, 16)
+
+    def listed(out, sc, lo, hi, src):
+        wrap(sc, lo, hi, src)
+        ts(out, wrapped(sc, hi, lo), R("up", 0, 1), Op.add)
 
     def engines(dst, a, b):
         m = 0
@@ -253,19 +256,21 @@ def rank_program(g, core, T, topo):
         for land, dst in pairs:
             rid, pid, _ = topo.addr(dst)
             ids.append(DstId(rid=rid, pnc=pid))
-        m = engines(pairs[0][1], 8, 12)
-        g.remote_dma_fused([RemoteDMATransfer(dst_ids=ids, dma_engine_mask=m, remote_sem=T.sem[sem], srcs=[T[src][:, :]],
-                                              dsts=[T[land][:, :] for land, dst in pairs])], local_sem=T.sem.sent)
-        total["sent"] = total.get("sent", 0) + 4
-        total[sem] = 4 * len(pairs)
+        ne = min(len(topo.engines(core, dst)) for land, dst in pairs)
+        g.remote_dma_fused([RemoteDMATransfer(dst_ids=ids, dma_engine_mask=engines(pairs[0][1], 0, ne), remote_sem=T.sem[sem],
+                                              srcs=[T[src][:, :]], dsts=[T[land][:, :] for land, dst in pairs])],
+                           local_sem=T.sem.sent)
+        total["sent"] = total.get("sent", 0) + ne
+        total[sem] = ne * len(pairs)
         for land, dst in pairs:
             hist.setdefault(land, []).append(((sem, total[sem], {}), "r", R(land)[1:], True))
 
     def load(q, out, src, sem, code=False):
         dma(q, lambda: queue[q].dma_start(ap(out).bitcast(dt.uint8) if code else ap(out), src), [], [out], sem)
-    load("s", R("xt", 0, 1024), T.x[:, 0:1024], "lx0")
     load("a", R("ut"), T.u[:, :], "ldu")
-    load("a", R("xt", 1024, 2048), T.x[:, 1024:2048], "lx1")
+    load("s", R("xt", 0, 1024), T.x[:, 0:1024], "lx0")
+    load("s", R("xt", 1024, 2048), T.x[:, 1024:2048], "lx1")
+    do_waits("s", needs("s", [R("xt")], []))
     load("s", R("qw"), T.wc[:, :], "lwc", code=True)
     load("s", R("sw"), T.ws[:, :], "lws")
     load("s", R("vt"), T.v[:, :], "ldv")
@@ -287,17 +292,18 @@ def rank_program(g, core, T, topo):
             lo = 16 * min(m for m in s if m != EQ) + 16 if len(s) == 4 else 0
             yield R(name, 4 * (at + lo), 4 * (at + w))
 
+    EARLY = [tile for tile in OT if EQ not in tile[2] and max(tile[2]) < 16]
+    LATE = [tile for tile in OT if tile not in EARLY]
     memset(R("ones"), 1.0)
-    iota(R("c16i"), [[16, 32]], 0, 0)
     iota(R("ii"), [[1, 32]], 128, -1)
     iota(R("pj"), [[0, 32]], 0, 1)
-    iota(R("c15"), [[0, 32], [1, 16]], 0, 0)
+    iota(R("c16i"), [[16, 32]], 0, 0)
     choose(R("blk"), R("ones", 0, 128), [[-16, 8], [0, 16]], Op.is_ge, 0, 1)
     choose(R("grp"), R("blk"), [[16, 8], [0, 16]], Op.is_ge, 15, -1)
+    for r in pads("of", LATE[-1:] + EARLY + LATE[:-1]):
+        fill(r, 0)
     for b in range(4):
         choose(R("ct0", 512 * b, 512 * b + 512), R("ones"), [[-1, 512]], Op.is_equal, b, 4)
-    for r in pads("of", OT[3:]):
-        fill(r, 0)
     iota(R("io"), [[1, 768]], 0, 0)
     for r in pads("pf", PT):
         fill(r, 0)
@@ -305,48 +311,37 @@ def rank_program(g, core, T, topo):
     fill(R("zero"), 0)
     fill(R("pb1"), 1)
 
+    memset(R("rst"), FAR)
+    memset(R("rst", 0, 512, 16), -FAR)
     ts(R("jj"), R("ii"), 15, Op.bitwise_and)
-    ts2(R("dm16"), R("jj", 0, 16), 0.0, Op.is_gt, -FAR, Op.mult)
     ts(R("ii"), R("pj"), 15, Op.bitwise_and)
+    ts2(R("dm16"), R("jj", 0, 16), 0.0, Op.is_gt, -FAR, Op.mult)
     copy(R("pju"), R("ii"))
-    copy(R("ex0"), R("c16i", 0, 8))
     act(R("dm"), R("dm16"), off=R("pju"))
-    act(R("rst"), R("c15"), fn=Fn.Sign)
-    act(R("rst"), R("rst"), scale=2 * FAR, bias=-FAR, fn=Fn.Identity)
+    copy(R("ex0"), R("c16i", 0, 8))
+    ts2(R("cwa"), R("jj", 0, 16), 0.0, Op.is_equal, 2 * DROP, Op.mult)
+    ts2(R("cwb"), R("jj", 0, 16), 1.0, Op.is_equal, -DROP, Op.mult)
+    ts2(R("up", 0, 1), R("ii", 0, 1), 15.0, Op.is_lt, DROP, Op.mult)
+    tt(R("cw16"), R("cwa"), R("cwb"), Op.add)
+    ts2(R("c16"), R("c16i"), R("up", 0, 1), Op.add, -1.0, Op.add)
     for t in range(4):
         act(R("ct1", t, 512, 4), R("grp"))
-    for t, k in ((0, 1.0), (1, 1.0), (2, 16.0), (3, 16.0)):
-        act(R("ct1", 512 + t, 1024, 4), R("grp"), scale=k)
-    for t, k in ((0, 0.0), (1, 0.0), (2, 1.0), (3, 1.0)):
-        act(R("ct1", 1024 + t, 1536, 4), R("grp"), scale=k)
-    for r in pads("of", OT[:3]):
-        memset(r, 0.0)
-    ts(R("c16"), R("c16i"), -1.0, Op.add)
-    memset(R("ors"), 0.0)
-    memset(R("prs"), 0.0)
+    act(R("cw"), R("cw16"), off=R("pju"))
+    memset(R("ors", 0, 1), 0.0)
+    memset(R("prs", 0, 1), 0.0)
     quant("u", "ut")
     op("v", lambda: g.vector.tensor_copy(T.qub[:, 0:128].bitcast(dt.uint32), T.qu[:, 0:128].bitcast(dt.uint32).indirect(T.ex0[:, 0:8])),
        [R("qu"), R("ex0")], [R("qub")])
     copy(R("sub"), R("su"), R("ex0"))
-    quant("x", "xt", 0, 256)
-    quant("x", "xt", 256, 256)
-    ts2(R("rsth"), R("c15"), 0.0, Op.is_gt, 2 * LOW, Op.mult)
 
     SC = {"o": "osc_", "p": "psc"}
-
-    def sort_begin(n, p, q, meanwhile=None):
-        mm(0, n, "ub", 0, q)
-        mm(1, n, "ub", 0, q)
-        if meanwhile:
-            meanwhile()
-        wrap(n, p + "mk", SC[p], src=ps(0, n), score=True)
 
     def scalar_of(p, m):
         return R(SC[p], 16 * m + 15, 16 * m + 16)
 
-    def compare(p, at, t, m):
+    def compare(p, at, t, m, bank=0):
         f = p + "f"
-        ts(R(f, 4 * at + t, 4 * (at + 16 * m + 16), 4), ps(0, 16 * m + 16), scalar_of(p, m), Op.is_gt)
+        ts(R(f, 4 * at + t, 4 * (at + 16 * m + 16), 4), ps(bank, 16 * m + 16), scalar_of(p, m), Op.is_gt)
         if m:
             act(R("junk", 512 * t, 512 * t + 16 * m), R(f, 4 * at + t, 4 * (at + 16 * m), 4), accum=R(p + "rs", m, m + 1))
 
@@ -359,64 +354,89 @@ def rank_program(g, core, T, topo):
     def equal(out, n, p):
         tt(out, R(SC[p], 0, n), ps(0, n), Op.is_equal)
 
+    def packed(p, tile):
+        quant(p + "f", p + "f", tile[0], tile[1])
+
+    def added(p, tile, first=False, last=False):
+        mm(2, tile[1], "c", 0, p + "f", m0=tile[0], start=first, stop=last)
+
     def summed(p, tile, first=False, last=False):
-        at, w, s = tile
-        f = p + "f"
-        quant(f, f, at, w)
-        mm(2, w, "c", 0, f, m0=at, start=first, stop=last)
+        packed(p, tile)
+        added(p, tile, first, last)
 
     def sort_end(n, p, rk, u16):
         tt(R(p + "rc"), R("c16", 0, n // 16), R(p + "rs"), Op.subtract)
-        wrap(n, p + "mk2", p + "sc2", src=ps(2, n))
+        wrap(p + "sc2", 0, n, ps(2, n))
         tt(R(rk), wrapped(p + "sc2", n), R(p + "rc"), Op.add)
         copy(R(u16), R(rk))
 
-    sort_begin(512, "o", "x")
+    where = {m: (tile[0], t) for tile in OT for t, m in enumerate(tile[2])}
     ahead = [m for ms in AHEAD.values() for m in ms]
-    for k, tile in enumerate(OT):
+    quant("x", "xt", 0, 256)
+    mm(3, 256, "ub", 0, "x")
+    quant("c", "ct1", 0, 128)
+    wrap_scores("omk", "osc_", 0, 256, ps(3, 256))
+    for m in range(15, -1, -1):
+        compare("o", where[m][0], where[m][1], m, bank=3)
+        if m == LOADED:
+            quant("x", "xt", 256, 256)
+            mm(0, 512, "ub", 0, "x")
+            mm(1, 512, "ub", 0, "x")
+        for tile in EARLY:
+            if m == min(tile[2]):
+                packed("o", tile)
+    wrap_scores("omk", "osc_", 256, 512, R("ps0", 256, 512))
+    for k, tile in enumerate(LATE):
         at, w, s = tile
+        for m in AHEAD.get(k, ()):
+            compare_scalar("o", where[m][0], where[m][1], m)
         for t, m in enumerate(s):
-            if m != EQ and m not in ahead:
+            if m >= 16 and m not in ahead:
                 compare("o", at, t, m)
         if EQ in s:
             equal(R("of", 4 * at + s.index(EQ), 4 * (at + 512), 4), 512, "o")
-        for m in AHEAD.get(k, ()):
-            l = [i for i, o in enumerate(OT) if m in o[2]][0]
-            compare_scalar("o", OT[l][0], OT[l][2].index(m), m)
+        summed("o", tile, first=k == 0, last=tile is LATE[-1])
         if k == 0:
-            quant("c", "ct1")
-        if k == 4:
-            act(R("dl"), R("dm"), scale=LOW / FAR)
-        summed("o", tile, first=k == 0, last=tile is OT[-1])
-    quant("e", "ct0")
-    for b in range(4):
-        mm(4 + b, 512, "e", 128 * b, "x")
+            for early in EARLY:
+                added("o", early)
+        if k == 1:
+            quant("e", "ct0")
+            for b in range(4):
+                mm(4 + b, 512, "e", 128 * b, "x")
     for b in range(4):
         act(R("th", 512 * b, 512 * b + 512), ps(4 + b, 512), scale=0.5)
     act(R("osr"), ps(1, 512))
     sort_end(512, "o", "rk", "rku")
     scatter(R("lst"), R("rku"), R("io", 0, 512))
-    wrap(512, "lmk", "lsc", src=R("lst", 0, 512, 2), src2=R("lst", 1, 512, 2))
-    copy(R("lu"), wrapped("lsc", 512))
 
-    def pair_up(z, win, even, odd, mid):
-        copy(mid(0), win(0), off=even)
-        for t in range(1, 4):
+    def pair_up(z, lst, offs, win, mid):
+        even, odd = R(offs, 0, 16), R(offs, 16, 32)
+        listed(even, "lsc", 0, 256, R(lst, 0, 512, 2))
+        for t in range(4):
             act(mid(t), win(t), off=even)
+        listed(odd, "lsc", 256, 512, R(lst, 1, 512, 2))
         for t in range(4):
             tt(R(z, t, 1024, 4), win(t), mid(t), Op.add, off=odd)
         quant(z, z)
 
-    pair_up("z1", lambda t: R("th", 512 * t, 512 * t + 512), R("lu", 0, 16), R("lu", 16, 32),
-            lambda t: R("h", 768 * t, 768 * t + 512, 2))
+    pair_up("z1", "lst", "lu", lambda t: R("th", 512 * t, 512 * t + 512), lambda t: R("h", 768 * t, 768 * t + 512, 2))
     send_mx("z1", "lz1", nxt, "rz1")
 
     for c in range(2):
         act(R("ssr", c, 512, 2), R("osr"), off=R("lu", 16 * c, 16 * c + 16))
-    wrap(512, "smk", "ssc", src=R("ssr"), score=True)
+    copy(R("rki"), R("rk"))
     memset(R("ww"), 9e29)
+    ts(R("rkh"), R("rki"), 1, Op.arith_shift_right)
+    for t, k in ((0, 1.0), (1, 1.0), (2, 16.0), (3, 16.0)):
+        ts(R("ct1", 512 + t, 1024, 4), R("grp"), k, Op.mult)
+    for t, k in ((0, 0.0), (1, 0.0), (2, 1.0), (3, 1.0)):
+        ts(R("ct1", 1024 + t, 1536, 4), R("grp"), k, Op.mult)
+    copy(R("rhu"), R("rkh"))
+    quant("c", "ct1", 128, 256)
+    quant("v", "vt")
+    wrap_scores("smk", "ssc", 0, 512, R("ssr"))
     copy(R("ww", 0, 32), wrapped("ssc", 512))
-    wrap(32, "pvm", "pvs", src=R("ssr", 15, 512, 16), score=True)
+    wrap_scores("pvm", "pvs", 0, 32, R("ssr", 15, 512, 16))
     for t in range(4):
         act(R("h", 768 * t + 1, 768 * t + 512, 2), R("th", 512 * t, 512 * t + 512), off=R("lu", 16, 32))
     iota(R("io2"), [[0, 2], [1, 256]], 0, 0)
@@ -438,11 +458,14 @@ def rank_program(g, core, T, topo):
             else:
                 act(R(tile, b, 1024, 4), ps(4 + b, 256), scale=0.03125)
 
-    def merge(t, need, first, second):
+    def merge(t, need, first, placed):
         s = str(t)
         layer("lz" + s, "pt")
         quant("p" + s, "pt")
-        sort_begin(256, "p", "p" + s, first)
+        mm(0, 256, "ub", 0, "p" + s)
+        mm(1, 256, "ub", 0, "p" + s)
+        first()
+        wrap_scores("pmk", "psc", 0, 256, ps(0, 256))
         act(R("psr"), ps(1, 256))
         for b in range(4):
             mm(4 + b, 256, "e", 128 * b, "p" + s)
@@ -455,8 +478,7 @@ def rank_program(g, core, T, topo):
         for k, m in enumerate(PT[1][2]):
             compare("p", PT[1][0], k, m)
         equal(R("aux", 0, 1024, 4), 256, "p")
-        wrap(256, "lmk", "lsc", src=ps(3, 256))
-        copy(R("segu"), wrapped("lsc", 256))
+        listed(R("segu"), "lsc", 0, 256, ps(3, 256))
         tt(R("aux", 1, 1024, 4), R("ww"), R("psr"), Op.is_le, off=R("segu"))
         quant("aux", "aux")
         mm(2, 256, "c", 128, "aux", start=True, stop=False)
@@ -468,97 +490,104 @@ def rank_program(g, core, T, topo):
         summed("p", PT[0], last=True)
         for b in range(4):
             act(R("h", 768 * b + 512, 768 * b + 768), ps(4 + b, 256), scale=0.5)
-        second()
         sort_end(256, "p", "pl" + s, "plu" + s)
+        placed()
         pb, ob, pl = R("pb" + s), R("ob" + s), R("plu" + s)
         scatter(pb, pl, R("zero", 0, 256))
         scan(R("ob" + s, 0, need), R("pb" + s, 0, need), R("zero", 0, need), -1.0, Op.add, Op.add)
         scatter(ob, pl, R("io", 512, 768))
 
     held = lambda t: R("h", 768 * t, 768 * t + 768)
-
-    def halved_ranks():
-        copy(R("rki"), R("rk"))
-        ts(R("rkh"), R("rki"), 1, Op.arith_shift_right)
-        copy(R("rhu"), R("rkh"))
-    merge(1, 512, lambda: quant("v", "vt"), halved_ranks)
-    wrap(512, "lmk", "lsc", src=R("ob1", 0, 512, 2), src2=R("ob1", 1, 512, 2))
-    copy(R("elu1"), wrapped("lsc", 512))
-    pair_up("z2", held, R("elu1", 0, 16), R("elu1", 16, 32), lambda t: R("mid", 256 * t, 256 * t + 256))
+    merge(1, 512, lambda: None, lambda: None)
+    pair_up("z2", "ob1", "elu1", held, lambda t: R("mid", 256 * t, 256 * t + 256))
     send_mx("z2", "lz2", nxt, "rz2")
 
+    scatter(R("at1"), R("elu1"), R("io2"))
     ts(R("pli"), R("pl1"), 512.0, Op.min)
     ts(R("plh"), R("pli"), 1, Op.arith_shift_right)
     copy(R("a1u"), R("plh"))
     send_list("a1u", [("la1", prv)], "ra1")
-    scatter(R("at1"), R("elu1"), R("io2"))
     fill(R("aux", 3, 1024, 4), 0)
     for t in range(4):
-        act(R("wm", 768 * t, 768 * t + 512), R("h", 768 * t, 768 * t + 512))
+        act(R("wm", 768 * t, 768 * t + 512), R("h", 768 * t, 768 * t + 512), scale=2.0)
+    act(R("gh"), R("at1"), off=R("rku"))
 
-    def mask_places():
-        tt(R("mkh"), R("at1"), R("dl"), Op.add, off=R("rku"))
-
-    def wrap_places():
-        scan(R("sch"), R("rsth"), R("mkh"), -FAR, Op.min, Op.max)
-        copy(R("h1u"), wrapped("sch", 512))
-    merge(2, 256, mask_places, wrap_places)
-    wrap(256, "lmk", "lsc", src=R("ob2", 0, 256))
-    copy(R("elu2"), wrapped("lsc", 256))
+    def send_places():
+        ts(R("a2u"), R("pl2"), 256.0, Op.min)
+        send_list("a2u", [("la2n", prv), ("la2m", prv2)], "ra2")
+    merge(2, 256, lambda: listed(R("h1u"), "sch", 0, 512, R("gh")), send_places)
+    listed(R("elu2"), "lsc", 0, 256, R("ob2", 0, 256))
+    act(R("ra", 0, 256), R("io", 0, 264), off=R("la2n"))
+    act(R("rb", 0, 256), R("io", 0, 264), off=R("la2m"))
     for t in (1, 0, 3, 2):
         if t % 2:
             act(R("et", t, 1024, 4), held(t), scale=2.0, off=R("elu2"))
         else:
             ts(R("et", t, 1024, 4), held(t), 2.0, Op.mult, off=R("elu2"))
     quant("et", "et")
-    ts(R("cut2"), R("pl2"), 256.0, Op.min)
-    copy(R("a2u"), R("cut2"))
-    send_list("a2u", [("la2n", prv), ("la2m", prv2)], "ra2")
+    act(R("rc", 0, 256), R("rb"), off=R("la1"))
     scatter(R("at2"), R("elu2"), R("io", 512, 768))
     layer("et", "v2")
     quant("v2", "v2")
     send_mx("v2", "lv2", prv, "rv2")
-    for b in range(4):
-        act(R("v2h", 256 * b, 256 * b + 256), ps(4 + b, 256), scale=0.03125 * 0.5)
-    act(R("ra", 0, 256), R("io", 0, 264), off=R("la2n"))
-    act(R("rb", 0, 256), R("io", 0, 264), off=R("la2m"))
-    act(R("rc", 0, 256), R("rb"), off=R("la1"))
-    wrap(512, "lmk", "lsc", win=R("at2"), off=R("rku"))
-    copy(R("p2u"), wrapped("lsc", 512))
-    ts(R("u2"), wrapped("lsc", 512), 512.0, Op.is_ge)
-    for t in range(4):
-        tt(R("wm", 768 * t + 512, 768 * t + 768), held(t), R("v2h", 256 * t, 256 * t + 256), Op.add, off=R("elu2"))
+    act(R("g2"), R("at2"), off=R("rku"))
+    act(R("g1"), R("ra"), off=R("h1u"))
 
+    def first_mean(t):
+        tt(R("wm", 768 * t + 512, 768 * t + 768), R("et", t, 1024, 4), R("v2", t, 1024, 4), Op.add)
+
+    def pick(t):
+        act(R("x2q", 512 * t, 512 * t + 512), R("wm", 768 * t, 768 * t + 768), scale=0.125, off=R("p2u"))
+
+    def second_mean(t):
+        tt(R("x1h", 512 * t, 512 * t + 512), R("d1q", 272 * t, 272 * t + 272), R("x2q", 512 * t, 512 * t + 512), Op.add, off=R("o1u"))
+    first_mean(0)
+    listed(R("p2u"), "sc2", 0, 512, R("g2"))
+    first_mean(1)
+    pick(0)
+    pick(1)
+    listed(R("o1u"), "sc1", 0, 512, R("g1"))
+    first_mean(2)
+    first_mean(3)
+    ts2(R("u2"), wrapped("sc2", 512), R("up", 0, 1), Op.add, 512.0, Op.is_ge)
+    ts2(R("u1"), wrapped("sc1", 512), R("up", 0, 1), Op.add, 256.0, Op.is_lt)
+    tt(R("ucs"), R("u2"), R("u1"), Op.add)
     for b in range(4):
         mm(4 + b, 256, "e", 128 * b, "lv2")
     for b in range(4):
-        act(R("d1", b, 1024, 4), ps(4 + b, 256))
-    wrap(512, "lmk", "lsc", win=R("ra"), off=R("h1u"))
-    copy(R("o1u"), wrapped("lsc", 512))
-    ts(R("u1"), wrapped("lsc", 512), 256.0, Op.is_lt)
+        if b % 2:
+            copy(R("d1", b, 1024, 4), ps(4 + b, 256))
+        else:
+            act(R("d1", b, 1024, 4), ps(4 + b, 256))
+        if b == 0:
+            act(R("d1q", 0, 256), ps(4, 256), scale=0.25)
+    for b in range(1, 4):
+        if b >= 2:
+            pick(b)
+        act(R("d1q", 272 * b, 272 * b + 256), ps(4 + b, 256), scale=0.25)
     quant("d1", "d1")
     send_mx("d1", "ld1", prv, "rd1")
-    for b in range(4):
-        act(R("d1q", 272 * b, 272 * b + 256), ps(4 + b, 256), scale=0.25)
-        act(R("x2q", 512 * b, 512 * b + 512), R("wm", 768 * b, 768 * b + 768), scale=0.25, off=R("p2u"))
-    wrap(512, "lmk", "lsc", win=R("rc"), off=R("rhu"))
-    copy(R("o0u"), wrapped("lsc", 512))
-    ts(R("u0"), wrapped("lsc", 512), 256.0, Op.is_lt)
+    act(R("g0"), R("rc"), off=R("rhu"))
     for t in range(4):
-        tt(R("x1h", 512 * t, 512 * t + 512), R("d1q", 272 * t, 272 * t + 272), R("x2q", 512 * t, 512 * t + 512), Op.add, off=R("o1u"))
-    tt(R("ucs"), R("u2"), R("u1"), Op.add)
-    tt(R("uct"), R("ucs"), R("u0"), Op.add)
-    copy(R("ucu"), R("uct"))
+        second_mean(t)
+    listed(R("o0u"), "sc0", 0, 512, R("g0"))
     for b in range(4):
         mm(b, 256, "e", 128 * b, "ld1")
     for b in range(4):
         act(R("d0h", 272 * b, 272 * b + 256), ps(b, 256), scale=0.5)
-    act(R("ucr"), R("io", 0, 16), off=R("ucu"))
-    dma("s", lambda: g.sync.dma_start(T.uc[:, :], T.ucr[0:128:16, :]), [R("ucr")], [], "sto")
+
+    def store_counts():
+        op("v", lambda: g.vector.transpose(ap(R("ucr")), ap(R("uct"))), [R("uct")], [R("ucr")])
+        for k in range(2):
+            dma("s", lambda: g.sync.dma_start(T.uc[k:8:2, :], T.ucr[:, 16 * k:16 * k + 16]), [R("ucr")], [], "sto")
+    counts = (lambda: ts2(R("u0"), wrapped("sc0", 512), R("up", 0, 1), Op.add, 256.0, Op.is_lt),
+              lambda: tt(R("uct"), R("ucs"), R("u0"), Op.add), store_counts)
     for c, (lo, hi) in enumerate(((0, 352), (352, 512))):
         for t in range(4):
             tt(R("xo", 4 * lo + t, 4 * hi, 4), R("d0h", 272 * t, 272 * t + 272), R("x1h", 512 * t + lo, 512 * t + hi), Op.add,
                off=R("o0u", lo // 16, hi // 16))
+            if c == 0 and t < 3:
+                counts[t]()
         quant("xo", "xo", lo, hi - lo)
         q = R("qxo", lo, hi)
         dma("s", lambda: g.sync.dma_start(T.oc[:, 4 * lo:4 * hi], ap(q).bitcast(dt.uint8)), [q], [], "sto")

@@ -34,8 +34,10 @@ def _mx(**kw):
 
 
 EQ = -1
-AHEAD = {0: [24, 20], 1: [16]}
+AHEAD = [24, 16]
+SCALARS = {1: 3, 2: 3}
 LOADED = 9
+CUT = 320
 
 
 def tiles_of(slots, n):
@@ -50,22 +52,22 @@ def tiles_of(slots, n):
 
 OT, OF = tiles_of([EQ] + list(range(31, -1, -1)), 512)
 PT, PF = tiles_of(list(range(15, -1, -1)), 256)
-_b(BF, xt=2048, ut=512, vt=512, ct0=2048, ct1=1536, ones=512, blk=128, grp=128,
+_b(BF, xt=2048, ut=512, vt=512, ct0=2048, ct1=1536, ones=128, unit=128, blk=128, grp=128,
    of=4 * OF, pf=4 * PF, junk=2048, aux=1024, at1=768, ra=272, rb=272, rc=272,
    th=2048, h=3072, wm=3072, mid=1024, z1=1024, z2=1024, pt=1024, et=1024, v2=1024, d1=1024,
-   d1q=1088, d0h=1088, x2q=2048, x1h=2048, xo=2048, rst=512, cw=512, gh=512, g1=512, g0=512)
-_b(F32, dm=512, dm16=16, cw16=16, zero=512, io=768, io2=512, osr=512, psr=256, qmk=512, osc_=512, psc=256,
+   d1q=1088, d0h=1088, x2q=2048, x1h=2048, xo=2048, rst=512, cw=512, cs=512)
+_pack("gathered", BF, gh=512, g1=512, g0=512)
+_b(F32, dm=512, dm16=16, cw16=16, io=768, io2=512, osr=512, psr=256, qmk=512, osc_=512, psc=256,
    lst=512, ssr=512, ssc=512, pvs=32, ww=40, pb1=768, pb2=768, ob1=768, ob2=768, at2=768, ucr=32, yo=512, g2=512)
-_b(F16, lsc=512, sch=512, sc2=512, sc1=512, sc0=512)
-_same("qmk", omk=512, pmk=256, smk=512, pvm=32)
-_same("lsc", osc2=512, psc2=256)
+_pack("scans", F16, lsc=512, sch=512, sc2=512, sc1=512, sc0=512)
+_same("qmk", omk=512, pmk=256)
+_same("scans", osc2=512, psc2=256)
 _pack("small", F32, c16=32, ors=32, orc=32, rk=32, prs=16, prc=16, pl1=16, pl2=16, u2=32, u1=32, u0=32, ucs=32, uct=32,
       cwa=16, cwb=16, up=8)
 _b(I32, ii=32, jj=32, pj=32)
 _pack("whole", I32, c16i=32, pli=16, plh=16, rki=32, rkh=32)
 _b(U16, ex0=8, pju=32, a1u=16, a2u=16, la1=16, la2n=16, la2m=16)
-_pack("offs", U16, rku=32, rhu=32, lu=32, segu=16, plu1=16, plu2=16, elu1=32, elu2=16, h1u=32, p2u=32, o1u=32,
-      o0u=32)
+_pack("offs", U16, rku=32, rhu=32, lu=32, segu=16, plu1=16, plu2=16, elu1=32, elu2=16, h1u=32, p2u=32, o1u=32, o0u=32)
 _mx(x=512, u=128, ub=128, v=128, w=512, e=512, c=384,
     z1=256, z2=256, lz1=256, lz2=256, p1=256, p2=256, et=256, v2=256, lv2=256, d1=256, ld1=256, xo=512)
 for _k, _d in (("q", F8), ("s", U8)):
@@ -216,9 +218,14 @@ def rank_program(g, core, T, topo):
     def ps(k, n):
         return R("ps%d" % k, 0, n)
 
-    def wrap_scores(mk, sc, lo, hi, src):
+    def mask(mk, lo, hi, src):
         tt(R(mk, lo, hi), src, R("dm", 0, hi - lo), Op.add)
+
+    def maxima(mk, sc, lo, hi):
         scan(R(sc, lo, hi), R("rst", 0, hi - lo), R(mk, lo, hi), -FAR, Op.min, Op.max)
+
+    def wrap_sorted(sc, n, src):
+        scan(R(sc, 0, n), R("cs", 0, n), src, -FAR, Op.add, Op.min)
 
     def wrap(sc, lo, hi, src):
         scan(R(sc, lo, hi), R("cw", 0, hi - lo), src, 0.0, Op.add, Op.min)
@@ -226,9 +233,15 @@ def rank_program(g, core, T, topo):
     def wrapped(sc, n, lo=0):
         return R(sc, lo + 15, n, 16)
 
-    def listed(out, sc, lo, hi, src):
-        wrap(sc, lo, hi, src)
+    def lifted(out, sc, lo, hi):
         ts(out, wrapped(sc, hi, lo), R("up", 0, 1), Op.add)
+
+    def weave(chain, between, lead=False):
+        between = list(between) + [None] * len(chain)
+        for f, o in zip(chain, between):
+            for call in ((o, f) if lead else (f, o)):
+                if call:
+                    call()
 
     def engines(dst, a, b):
         m = 0
@@ -298,41 +311,46 @@ def rank_program(g, core, T, topo):
     iota(R("ii"), [[1, 32]], 128, -1)
     iota(R("pj"), [[0, 32]], 0, 1)
     iota(R("c16i"), [[16, 32]], 0, 0)
-    choose(R("blk"), R("ones", 0, 128), [[-16, 8], [0, 16]], Op.is_ge, 0, 1)
+    choose(R("unit"), R("ones"), [[-1, 128]], Op.is_equal, 0, 1)
+    choose(R("blk"), R("ones"), [[-16, 8], [0, 16]], Op.is_ge, 0, 1)
     choose(R("grp"), R("blk"), [[16, 8], [0, 16]], Op.is_ge, 15, -1)
     for r in pads("of", LATE[-1:] + EARLY + LATE[:-1]):
         fill(r, 0)
-    for b in range(4):
-        choose(R("ct0", 512 * b, 512 * b + 512), R("ones"), [[-1, 512]], Op.is_equal, b, 4)
     iota(R("io"), [[1, 768]], 0, 0)
     for r in pads("pf", PT):
         fill(r, 0)
     fill(R("aux"), 0)
-    fill(R("zero"), 0)
     fill(R("pb1"), 1)
+    iota(R("io2"), [[0, 2], [1, 256]], 0, 0)
+    fill(R("at1"), 256)
 
-    memset(R("rst"), FAR)
-    memset(R("rst", 0, 512, 16), -FAR)
+    memset(R("ct0", 0, 1024), 0.0)
     ts(R("jj"), R("ii"), 15, Op.bitwise_and)
+    memset(R("rst"), FAR)
     ts(R("ii"), R("pj"), 15, Op.bitwise_and)
     ts2(R("dm16"), R("jj", 0, 16), 0.0, Op.is_gt, -FAR, Op.mult)
+    memset(R("rst", 0, 512, 16), -FAR)
     copy(R("pju"), R("ii"))
     act(R("dm"), R("dm16"), off=R("pju"))
+    memset(R("ct0", 1024, 2048), 0.0)
     copy(R("ex0"), R("c16i", 0, 8))
-    ts2(R("cwa"), R("jj", 0, 16), 0.0, Op.is_equal, 2 * DROP, Op.mult)
-    ts2(R("cwb"), R("jj", 0, 16), 1.0, Op.is_equal, -DROP, Op.mult)
-    ts2(R("up", 0, 1), R("ii", 0, 1), 15.0, Op.is_lt, DROP, Op.mult)
-    tt(R("cw16"), R("cwa"), R("cwb"), Op.add)
-    ts2(R("c16"), R("c16i"), R("up", 0, 1), Op.add, -1.0, Op.add)
-    for t in range(4):
-        act(R("ct1", t, 512, 4), R("grp"))
-    act(R("cw"), R("cw16"), off=R("pju"))
+    for b in range(4):
+        copy(R("ct0", 512 * b + b, 512 * b + 512, 4), R("unit"))
+    zeros = R("ct0", 3, 1024, 4)
     memset(R("ors", 0, 1), 0.0)
     memset(R("prs", 0, 1), 0.0)
     quant("u", "ut")
+    ts2(R("cwa"), R("jj", 0, 16), 0.0, Op.is_equal, 2 * DROP, Op.mult)
+    ts2(R("cwb"), R("jj", 0, 16), 1.0, Op.is_equal, -DROP, Op.mult)
     op("v", lambda: g.vector.tensor_copy(T.qub[:, 0:128].bitcast(dt.uint32), T.qu[:, 0:128].bitcast(dt.uint32).indirect(T.ex0[:, 0:8])),
        [R("qu"), R("ex0")], [R("qub")])
-    copy(R("sub"), R("su"), R("ex0"))
+    for t in range(4):
+        act(R("ct1", t, 512, 4), R("grp"))
+    act(R("sub"), R("su"), off=R("ex0"))
+    for t, k in ((0, 1.0), (1, 1.0), (2, 16.0), (3, 16.0)):
+        act(R("ct1", 512 + t, 1024, 4), R("grp"), scale=k)
+    for t, k in ((0, 0.0), (1, 0.0), (2, 1.0), (3, 1.0)):
+        act(R("ct1", 1024 + t, 1536, 4), R("grp"), scale=k)
 
     SC = {"o": "osc_", "p": "psc"}
 
@@ -345,11 +363,14 @@ def rank_program(g, core, T, topo):
         if m:
             act(R("junk", 512 * t, 512 * t + 16 * m), R(f, 4 * at + t, 4 * (at + 16 * m), 4), accum=R(p + "rs", m, m + 1))
 
-    def compare_scalar(p, at, t, m):
-        f, k = p + "f", 512 * t
-        act(R("junk", k, k + 16 * m + 16), ps(1, 16 * m + 16), fn=Fn.Sign, scale=-1.0, bias=scalar_of(p, m))
-        act(R(f, 4 * at + t, 4 * (at + 16 * m), 4), R("junk", k, k + 16 * m), fn=Fn.Relu, scale=-1.0, accum=R(p + "rs", m, m + 1))
-        act(R(f, 4 * (at + 16 * m) + t, 4 * (at + 16 * m + 16), 4), R("junk", k + 16 * m, k + 16 * m + 16), fn=Fn.Relu, scale=-1.0)
+    def compare_scalar(p, steps):
+        f = p + "f"
+        for k, (at, t, m) in enumerate(steps):
+            act(R("junk", 512 * k, 512 * k + 16 * m + 16), ps(1, 16 * m + 16), fn=Fn.Sign, scale=-1.0, bias=scalar_of(p, m))
+        for k, (at, t, m) in enumerate(steps):
+            j = 512 * k + 16 * m
+            act(R(f, 4 * at + t, 4 * (at + 16 * m), 4), R("junk", 512 * k, j), fn=Fn.Relu, scale=-1.0, accum=R(p + "rs", m, m + 1))
+            act(R(f, 4 * (at + 16 * m) + t, 4 * (at + 16 * m + 16), 4), R("junk", j, j + 16), fn=Fn.Relu, scale=-1.0)
 
     def equal(out, n, p):
         tt(out, R(SC[p], 0, n), ps(0, n), Op.is_equal)
@@ -364,83 +385,84 @@ def rank_program(g, core, T, topo):
         packed(p, tile)
         added(p, tile, first, last)
 
-    def sort_end(n, p, rk, u16):
-        tt(R(p + "rc"), R("c16", 0, n // 16), R(p + "rs"), Op.subtract)
-        wrap(p + "sc2", 0, n, ps(2, n))
-        tt(R(rk), wrapped(p + "sc2", n), R(p + "rc"), Op.add)
-        copy(R(u16), R(rk))
+    def sort_end(n, p, rk, u16, *between):
+        weave([lambda: tt(R(p + "rc"), R("c16", 0, n // 16), R(p + "rs"), Op.subtract),
+               lambda: wrap(p + "sc2", 0, n, ps(2, n)),
+               lambda: tt(R(rk), wrapped(p + "sc2", n), R(p + "rc"), Op.add),
+               lambda: copy(R(u16), R(rk))], (None,) + between)
 
     where = {m: (tile[0], t) for tile in OT for t, m in enumerate(tile[2])}
-    ahead = [m for ms in AHEAD.values() for m in ms]
     quant("x", "xt", 0, 256)
     mm(3, 256, "ub", 0, "x")
-    quant("c", "ct1", 0, 128)
-    wrap_scores("omk", "osc_", 0, 256, ps(3, 256))
+    quant("e", "ct0", 0, 256)
+    ts2(R("up", 0, 1), R("ii", 0, 1), 15.0, Op.is_lt, DROP, Op.mult)
+    tt(R("cw16"), R("cwa"), R("cwb"), Op.add)
+    ts2(R("c16"), R("c16i"), R("up", 0, 1), Op.add, -1.0, Op.add)
+    act(R("cw"), R("cw16"), off=R("pju"))
+    mask("omk", 0, 256, ps(3, 256))
+    quant("e", "ct0", 256, 128)
+    maxima("omk", "osc_", 0, 256)
+    quant("e", "ct0", 384, 128)
     for m in range(15, -1, -1):
         compare("o", where[m][0], where[m][1], m, bank=3)
         if m == LOADED:
             quant("x", "xt", 256, 256)
             mm(0, 512, "ub", 0, "x")
             mm(1, 512, "ub", 0, "x")
-        for tile in EARLY:
-            if m == min(tile[2]):
-                packed("o", tile)
-    wrap_scores("omk", "osc_", 256, 512, R("ps0", 256, 512))
-    for k, tile in enumerate(LATE):
-        at, w, s = tile
-        for m in AHEAD.get(k, ()):
-            compare_scalar("o", where[m][0], where[m][1], m)
-        for t, m in enumerate(s):
-            if m >= 16 and m not in ahead:
-                compare("o", at, t, m)
-        if EQ in s:
-            equal(R("of", 4 * at + s.index(EQ), 4 * (at + 512), 4), 512, "o")
-        summed("o", tile, first=k == 0, last=tile is LATE[-1])
-        if k == 0:
-            for early in EARLY:
-                added("o", early)
-        if k == 1:
-            quant("e", "ct0")
             for b in range(4):
                 mm(4 + b, 512, "e", 128 * b, "x")
+        for tile in EARLY[:-1]:
+            if m == min(tile[2]) - 1:
+                packed("o", tile)
+        if m == 2:
+            mask("omk", 256, 512, R("ps0", 256, 512))
+        if m == 1:
+            maxima("omk", "osc_", 256, 512)
+    quant("c", "ct1", 0, 128)
+    packed("o", EARLY[-1])
+    compare_scalar("o", [where[m] + (m,) for m in AHEAD])
+    for k, (at, w, s) in enumerate(LATE[:-1]):
+        for i, m in enumerate(m for m in s if m not in AHEAD):
+            if m == EQ:
+                equal(R("of", 4 * at + s.index(EQ), 4 * (at + 512), 4), 512, "o")
+            else:
+                compare("o", at, where[m][1], m)
+            if i == 0 and k > 0:
+                summed("o", LATE[k - 1], first=k == 1)
+                for early in EARLY if k == 1 else ():
+                    added("o", early)
+    summed("o", LATE[-1])
+    summed("o", LATE[-2], last=True)
     for b in range(4):
         act(R("th", 512 * b, 512 * b + 512), ps(4 + b, 512), scale=0.5)
     act(R("osr"), ps(1, 512))
-    sort_end(512, "o", "rk", "rku")
+    act(R("cs"), R("dm"), fn=Fn.Identity, scale=2.0, bias=2 * FAR)
+    quant("c", "ct1", 128, 256)
+    sort_end(512, "o", "rk", "rku", lambda: quant("v", "vt"), lambda: memset(R("ww"), 9e29), lambda: copy(R("rki"), R("rk")))
     scatter(R("lst"), R("rku"), R("io", 0, 512))
 
-    def pair_up(z, lst, offs, win, mid):
+    def pair_up(z, lst, offs, win, mid, *between):
         even, odd = R(offs, 0, 16), R(offs, 16, 32)
-        listed(even, "lsc", 0, 256, R(lst, 0, 512, 2))
-        for t in range(4):
+        weave([lambda: wrap("lsc", 0, 256, R(lst, 0, 512, 2))], between[:1], lead=True)
+        wrap("lsc", 256, 512, R(lst, 1, 512, 2))
+        lifted(even, "lsc", 0, 256)
+        lifted(odd, "lsc", 256, 512)
+        copy(mid(3), win(3), off=even)
+        for t in range(3):
             act(mid(t), win(t), off=even)
-        listed(odd, "lsc", 256, 512, R(lst, 1, 512, 2))
-        for t in range(4):
+        for t in (3, 0, 1, 2):
             tt(R(z, t, 1024, 4), win(t), mid(t), Op.add, off=odd)
-        quant(z, z)
+        weave([lambda: quant(z, z)], between[1:], lead=True)
+        send_mx(z, "l" + z, nxt, "r" + z)
 
-    pair_up("z1", "lst", "lu", lambda t: R("th", 512 * t, 512 * t + 512), lambda t: R("h", 768 * t, 768 * t + 512, 2))
-    send_mx("z1", "lz1", nxt, "rz1")
+    pair_up("z1", "lst", "lu", lambda t: R("th", 512 * t, 512 * t + 512), lambda t: R("h", 768 * t, 768 * t + 512, 2),
+            lambda: ts(R("rkh"), R("rki"), 1, Op.arith_shift_right), lambda: copy(R("rhu"), R("rkh")))
 
     for c in range(2):
         act(R("ssr", c, 512, 2), R("osr"), off=R("lu", 16 * c, 16 * c + 16))
-    copy(R("rki"), R("rk"))
-    memset(R("ww"), 9e29)
-    ts(R("rkh"), R("rki"), 1, Op.arith_shift_right)
-    for t, k in ((0, 1.0), (1, 1.0), (2, 16.0), (3, 16.0)):
-        ts(R("ct1", 512 + t, 1024, 4), R("grp"), k, Op.mult)
-    for t, k in ((0, 0.0), (1, 0.0), (2, 1.0), (3, 1.0)):
-        ts(R("ct1", 1024 + t, 1536, 4), R("grp"), k, Op.mult)
-    copy(R("rhu"), R("rkh"))
-    quant("c", "ct1", 128, 256)
-    quant("v", "vt")
-    wrap_scores("smk", "ssc", 0, 512, R("ssr"))
+    wrap_sorted("ssc", 512, R("ssr"))
+    wrap_sorted("pvs", 32, R("ssr", 15, 512, 16))
     copy(R("ww", 0, 32), wrapped("ssc", 512))
-    wrap_scores("pvm", "pvs", 0, 32, R("ssr", 15, 512, 16))
-    for t in range(4):
-        act(R("h", 768 * t + 1, 768 * t + 512, 2), R("th", 512 * t, 512 * t + 512), off=R("lu", 16, 32))
-    iota(R("io2"), [[0, 2], [1, 256]], 0, 0)
-    fill(R("at1"), 256)
     fill(R("pb2"), 1)
     iota(R("at2"), [[1, 768]], 0, 0)
     for b in ("ra", "rb", "rc"):
@@ -449,89 +471,109 @@ def rank_program(g, core, T, topo):
         for t in range(4):
             fill(R(b, 272 * t + 256, 272 * t + 272), 0)
 
-    def layer(q, tile):
+    def layer(q, tile, on_vector=(1, 3)):
         for b in range(4):
             mm(4 + b, 256, "w", 128 * b, q)
         for b in range(4):
-            if b % 2:
+            if b in on_vector:
                 ts(R(tile, b, 1024, 4), ps(4 + b, 256), 0.03125, Op.mult)
             else:
                 act(R(tile, b, 1024, 4), ps(4 + b, 256), scale=0.03125)
 
-    def merge(t, need, first, placed):
+    def merge(t, need, sorted_, between):
         s = str(t)
         layer("lz" + s, "pt")
         quant("p" + s, "pt")
         mm(0, 256, "ub", 0, "p" + s)
         mm(1, 256, "ub", 0, "p" + s)
-        first()
-        wrap_scores("pmk", "psc", 0, 256, ps(0, 256))
+        steps = [(tile[0], k, m) for tile in PT for k, m in enumerate(tile[2])]
+        mine = iter(steps[SCALARS[t]:])
+
+        def step(n=1):
+            for _ in range(n):
+                compare("p", *next(mine))
+
+        def pivot(k):
+            ts(R("aux", 2 + k, 1024, 4), ps(0, 256), R("pvs", 16 * k + 15, 16 * k + 16), Op.is_ge)
+        mask("pmk", 0, 256, ps(0, 256))
+        pivot(0)
+        maxima("pmk", "psc", 0, 256)
+        if need > 256:
+            pivot(1)
+        else:
+            quant("seg", "aux")
         act(R("psr"), ps(1, 256))
+        compare_scalar("p", steps[:SCALARS[t]])
+        step()
+        if need > 256:
+            quant("seg", "aux")
+        mm(3, 256, "c", 256, "seg")
         for b in range(4):
             mm(4 + b, 256, "e", 128 * b, "p" + s)
-        for k, m in enumerate(PT[0][2]):
-            compare_scalar("p", PT[0][0], k, m)
-        for k in range(need // 256):
-            ts(R("aux", 2 + k, 1024, 4), ps(0, 256), R("pvs", 16 * k + 15, 16 * k + 16), Op.is_ge)
-        quant("seg", "aux")
-        mm(3, 256, "c", 256, "seg")
-        for k, m in enumerate(PT[1][2]):
-            compare("p", PT[1][0], k, m)
+        step(7 - SCALARS[t])
         equal(R("aux", 0, 1024, 4), 256, "p")
-        listed(R("segu"), "lsc", 0, 256, ps(3, 256))
+        wrap("lsc", 0, 256, ps(3, 256))
+        packed("p", PT[1])
+        lifted(R("segu"), "lsc", 0, 256)
+        step()
         tt(R("aux", 1, 1024, 4), R("ww"), R("psr"), Op.is_le, off=R("segu"))
+        step()
         quant("aux", "aux")
         mm(2, 256, "c", 128, "aux", start=True, stop=False)
-        summed("p", PT[1])
-        for tile in PT[2:]:
-            for k, m in enumerate(tile[2]):
-                compare("p", tile[0], k, m)
-            summed("p", tile)
-        summed("p", PT[0], last=True)
+        added("p", PT[1])
+        step(3)
+        summed("p", PT[2])
+        step(3)
+        summed("p", PT[0])
+        summed("p", PT[3], last=True)
         for b in range(4):
             act(R("h", 768 * b + 512, 768 * b + 768), ps(4 + b, 256), scale=0.5)
+        sorted_()
         sort_end(256, "p", "pl" + s, "plu" + s)
-        placed()
         pb, ob, pl = R("pb" + s), R("ob" + s), R("plu" + s)
-        scatter(pb, pl, R("zero", 0, 256))
-        scan(R("ob" + s, 0, need), R("pb" + s, 0, need), R("zero", 0, need), -1.0, Op.add, Op.add)
-        scatter(ob, pl, R("io", 512, 768))
+        weave([lambda: scatter(pb, pl, zeros),
+               lambda: scan(R("ob" + s, 0, need), R("pb" + s, 0, need), R("io", 0, need), -1.0, Op.add, Op.min),
+               lambda: scatter(ob, pl, R("io", 512, 768))], between, lead=True)
 
     held = lambda t: R("h", 768 * t, 768 * t + 768)
-    merge(1, 512, lambda: None, lambda: None)
+
+    def odd_columns():
+        for t in range(4):
+            act(R("h", 768 * t + 1, 768 * t + 512, 2), R("th", 512 * t, 512 * t + 512), off=R("lu", 16, 32))
+    merge(1, 512, odd_columns,
+          [lambda: ts(R("pli"), R("pl1"), 512.0, Op.min), lambda: ts(R("plh"), R("pli"), 1, Op.arith_shift_right),
+           lambda: copy(R("a1u"), R("plh"))])
     pair_up("z2", "ob1", "elu1", held, lambda t: R("mid", 256 * t, 256 * t + 256))
-    send_mx("z2", "lz2", nxt, "rz2")
+    send_list("a1u", [("la1", prv)], "ra1")
 
     scatter(R("at1"), R("elu1"), R("io2"))
-    ts(R("pli"), R("pl1"), 512.0, Op.min)
-    ts(R("plh"), R("pli"), 1, Op.arith_shift_right)
-    copy(R("a1u"), R("plh"))
-    send_list("a1u", [("la1", prv)], "ra1")
     fill(R("aux", 3, 1024, 4), 0)
     for t in range(4):
         act(R("wm", 768 * t, 768 * t + 512), R("h", 768 * t, 768 * t + 512), scale=2.0)
-    act(R("gh"), R("at1"), off=R("rku"))
 
     def send_places():
         ts(R("a2u"), R("pl2"), 256.0, Op.min)
         send_list("a2u", [("la2n", prv), ("la2m", prv2)], "ra2")
-    merge(2, 256, lambda: listed(R("h1u"), "sch", 0, 512, R("gh")), send_places)
-    listed(R("elu2"), "lsc", 0, 256, R("ob2", 0, 256))
-    act(R("ra", 0, 256), R("io", 0, 264), off=R("la2n"))
+    merge(2, 256, lambda: act(R("gh"), R("at1"), off=R("rku")), [send_places, None, lambda: wrap("sch", 0, 512, R("gh"))])
+    lifted(R("h1u"), "sch", 0, 512)
+    wrap("lsc", 0, 256, R("ob2", 0, 256))
+    lifted(R("elu2"), "lsc", 0, 256)
     act(R("rb", 0, 256), R("io", 0, 264), off=R("la2m"))
+    act(R("ra", 0, 256), R("io", 0, 264), off=R("la2n"))
+    act(R("rc", 0, 256), R("rb"), off=R("la1"))
     for t in (1, 0, 3, 2):
         if t % 2:
             act(R("et", t, 1024, 4), held(t), scale=2.0, off=R("elu2"))
         else:
             ts(R("et", t, 1024, 4), held(t), 2.0, Op.mult, off=R("elu2"))
     quant("et", "et")
-    act(R("rc", 0, 256), R("rb"), off=R("la1"))
+    act(R("g1"), R("ra"), off=R("h1u"))
     scatter(R("at2"), R("elu2"), R("io", 512, 768))
-    layer("et", "v2")
+    layer("et", "v2", (2, 3))
+    act(R("g2"), R("at2"), off=R("rku"))
     quant("v2", "v2")
     send_mx("v2", "lv2", prv, "rv2")
-    act(R("g2"), R("at2"), off=R("rku"))
-    act(R("g1"), R("ra"), off=R("h1u"))
+    act(R("g0"), R("rc"), off=R("rhu"))
 
     def first_mean(t):
         tt(R("wm", 768 * t + 512, 768 * t + 768), R("et", t, 1024, 4), R("v2", t, 1024, 4), Op.add)
@@ -541,53 +583,54 @@ def rank_program(g, core, T, topo):
 
     def second_mean(t):
         tt(R("x1h", 512 * t, 512 * t + 512), R("d1q", 272 * t, 272 * t + 272), R("x2q", 512 * t, 512 * t + 512), Op.add, off=R("o1u"))
+
+    def used(out, sc, bound, o):
+        ts2(R(out), wrapped(sc, 512), R("up", 0, 1), Op.add, bound, o)
+    wrap("sc1", 0, 512, R("g1"))
+    wrap("sc2", 0, 512, R("g2"))
     first_mean(0)
-    listed(R("p2u"), "sc2", 0, 512, R("g2"))
-    first_mean(1)
+    lifted(R("p2u"), "sc2", 0, 512)
     pick(0)
-    pick(1)
-    listed(R("o1u"), "sc1", 0, 512, R("g1"))
-    first_mean(2)
-    first_mean(3)
-    ts2(R("u2"), wrapped("sc2", 512), R("up", 0, 1), Op.add, 512.0, Op.is_ge)
-    ts2(R("u1"), wrapped("sc1", 512), R("up", 0, 1), Op.add, 256.0, Op.is_lt)
-    tt(R("ucs"), R("u2"), R("u1"), Op.add)
+    for t in range(1, 4):
+        first_mean(t)
     for b in range(4):
         mm(4 + b, 256, "e", 128 * b, "lv2")
     for b in range(4):
-        if b % 2:
+        if b >= 2:
             copy(R("d1", b, 1024, 4), ps(4 + b, 256))
         else:
             act(R("d1", b, 1024, 4), ps(4 + b, 256))
-        if b == 0:
-            act(R("d1q", 0, 256), ps(4, 256), scale=0.25)
-    for b in range(1, 4):
-        if b >= 2:
-            pick(b)
-        act(R("d1q", 272 * b, 272 * b + 256), ps(4 + b, 256), scale=0.25)
+    lifted(R("o1u"), "sc1", 0, 512)
+    used("u2", "sc2", 512.0, Op.is_ge)
+    used("u1", "sc1", 256.0, Op.is_lt)
     quant("d1", "d1")
     send_mx("d1", "ld1", prv, "rd1")
-    act(R("g0"), R("rc"), off=R("rhu"))
-    for t in range(4):
-        second_mean(t)
-    listed(R("o0u"), "sc0", 0, 512, R("g0"))
+    for b in range(4):
+        act(R("d1q", 272 * b, 272 * b + 256), ps(4 + b, 256), scale=0.25)
+        if b < 3:
+            pick(b + 1)
     for b in range(4):
         mm(b, 256, "e", 128 * b, "ld1")
     for b in range(4):
         act(R("d0h", 272 * b, 272 * b + 256), ps(b, 256), scale=0.5)
+    for t in range(3):
+        second_mean(t)
+    tt(R("ucs"), R("u2"), R("u1"), Op.add)
+    wrap("sc0", 0, 512, R("g0"))
+    second_mean(3)
+    lifted(R("o0u"), "sc0", 0, 512)
+    used("u0", "sc0", 256.0, Op.is_lt)
 
     def store_counts():
         op("v", lambda: g.vector.transpose(ap(R("ucr")), ap(R("uct"))), [R("uct")], [R("ucr")])
         for k in range(2):
             dma("s", lambda: g.sync.dma_start(T.uc[k:8:2, :], T.ucr[:, 16 * k:16 * k + 16]), [R("ucr")], [], "sto")
-    counts = (lambda: ts2(R("u0"), wrapped("sc0", 512), R("up", 0, 1), Op.add, 256.0, Op.is_lt),
-              lambda: tt(R("uct"), R("ucs"), R("u0"), Op.add), store_counts)
-    for c, (lo, hi) in enumerate(((0, 352), (352, 512))):
-        for t in range(4):
-            tt(R("xo", 4 * lo + t, 4 * hi, 4), R("d0h", 272 * t, 272 * t + 272), R("x1h", 512 * t + lo, 512 * t + hi), Op.add,
-               off=R("o0u", lo // 16, hi // 16))
-            if c == 0 and t < 3:
-                counts[t]()
+
+    def last_mean(t, lo, hi):
+        tt(R("xo", 4 * lo + t, 4 * hi, 4), R("d0h", 272 * t, 272 * t + 272), R("x1h", 512 * t + lo, 512 * t + hi), Op.add,
+           off=R("o0u", lo // 16, hi // 16))
+
+    def store(c, lo, hi):
         quant("xo", "xo", lo, hi - lo)
         q = R("qxo", lo, hi)
         dma("s", lambda: g.sync.dma_start(T.oc[:, 4 * lo:4 * hi], ap(q).bitcast(dt.uint8)), [q], [], "sto")
@@ -597,6 +640,14 @@ def rank_program(g, core, T, topo):
             dma(e, lambda: queue[e].dma_start(o, i), [R("sxo", lo, hi)], [], "sto" if e == "s" else "sty")
         act(R("yo", lo, hi), ps(4 + c, hi - lo))
         dma("a", lambda: g.scalar.dma_start(T.y[:, lo:hi], T.yo[:, lo:hi]), [R("yo", lo, hi)], [], "sty")
+    for t in range(4):
+        last_mean(t, 0, CUT)
+    tt(R("uct"), R("ucs"), R("u0"), Op.add)
+    store(0, 0, CUT)
+    for t in range(4):
+        last_mean(t, CUT, 512)
+    store_counts()
+    store(1, CUT, 512)
 
     for s in SEMAPHORES:
         if total.get(s, 0):

@@ -1,5 +1,5 @@
 from concourse.bass import DstId, RemoteDMATransfer
-from concourse.mybir import dt, AluOpType as Op, ActivationFunctionType as Fn
+from concourse.mybir import dt, AluOpType as Op, ActivationFunctionType as Fn, AxisListType
 
 F8, U8, BF, F32, I32, U16, F16 = "float8_e4m3fn_x4", "uint8", "bfloat16", "float32", "int32", "uint16", "float16"
 FAR = 4e29
@@ -33,10 +33,11 @@ def _mx(**kw):
         _b(U8, **{"s" + k: kw[k]})
 
 
-EQ = -1
-AHEAD = [24, 16]
+EQ, SEGMENT, PIVOTS = -1, -2, [-3, -4]
+AHEAD = [28, 24, 20, 16]
 SCALARS = {1: 3, 2: 3}
-LOADED = 9
+SHORT = {"o": 4, "p": 4}
+LOADED = 14
 CUT = 320
 
 
@@ -44,26 +45,27 @@ def tiles_of(slots, n):
     out, at = [], 0
     for k in range(0, len(slots), 4):
         s = slots[k:k + 4]
-        w = max(128, n if EQ in s else 16 * max(s) + 16)
+        w = max(128, n if min(s) < 0 else 16 * max(s) + 16)
         out.append((at, w, s))
         at += w
     return out, at
 
 
 OT, OF = tiles_of([EQ] + list(range(31, -1, -1)), 512)
-PT, PF = tiles_of(list(range(15, -1, -1)), 256)
+PT, PF = tiles_of([15, 14, 13, 12, EQ, SEGMENT] + list(range(11, 1, -1)) + PIVOTS + [1, 0], 256)
 _b(BF, xt=2048, ut=512, vt=512, ct0=2048, ct1=1536, ones=128, unit=128, blk=128, grp=128,
-   of=4 * OF, pf=4 * PF, junk=2048, aux=1024, at1=768, ra=272, rb=272, rc=272,
+   of=4 * OF, pf=4 * PF, junk=2048, at1=768, ra=272, rb=272, rc=272,
    th=2048, h=3072, wm=3072, mid=1024, z1=1024, z2=1024, pt=1024, et=1024, v2=1024, d1=1024,
-   d1q=1088, d0h=1088, x2q=2048, x1h=2048, xo=2048, rst=512, cw=512, cs=512)
-_pack("gathered", BF, gh=512, g1=512, g0=512)
-_b(F32, dm=512, dm16=16, cw16=16, io=768, io2=512, osr=512, psr=256, qmk=512, osc_=512, psc=256,
-   lst=512, ssr=512, ssc=512, pvs=32, ww=40, pb1=768, pb2=768, ob1=768, ob2=768, at2=768, ucr=32, yo=512, g2=512)
-_pack("scans", F16, lsc=512, sch=512, sc2=512, sc1=512, sc0=512)
+   d1q=1088, d0h=1088, x2q=2048, x1h=2048, xo=2048, rst=512, cw=512, cs=512, pb1=768, pb2=768, fl=512,
+   io=528, io2=512, lst=512, at2=768)
+_pack("gathered", BF, gh=512, g2=512, g1=512, g0=512)
+_b(F32, dm=512, dm16=16, cw16=16, osr=512, psr=256, qmk=512, osc_=512, psc=256,
+   ssr=512, ssc=528, pvs=32, ucr=32, yo=512)
+_pack("scans", F16, lsc=512, sch=512, sc2=512, sc1=512, sc0=512, ob=512, sco=512)
 _same("qmk", omk=512, pmk=256)
 _same("scans", osc2=512, psc2=256)
 _pack("small", F32, c16=32, ors=32, orc=32, rk=32, prs=16, prc=16, pl1=16, pl2=16, u2=32, u1=32, u0=32, ucs=32, uct=32,
-      cwa=16, cwb=16, up=8)
+      cwa=16, cwb=16, up=8, lm=32, rkm=32, pm=32)
 _b(I32, ii=32, jj=32, pj=32)
 _pack("whole", I32, c16i=32, pli=16, plh=16, rki=32, rkh=32)
 _b(U16, ex0=8, pju=32, a1u=16, a2u=16, la1=16, la2n=16, la2m=16)
@@ -71,7 +73,7 @@ _pack("offs", U16, rku=32, rhu=32, lu=32, segu=16, plu1=16, plu2=16, elu1=32, el
 _mx(x=512, u=128, ub=128, v=128, w=512, e=512, c=384,
     z1=256, z2=256, lz1=256, lz2=256, p1=256, p2=256, et=256, v2=256, lv2=256, d1=256, ld1=256, xo=512)
 for _k, _d in (("q", F8), ("s", U8)):
-    _pack(_k + "flags", _d, **{_k + "of": OF, _k + "pf": PF, _k + "seg": 256, _k + "aux": 256})
+    _pack(_k + "flags", _d, **{_k + "of": OF, _k + "pf": PF})
 for _k in range(8):
     SCRATCH["ps%d" % _k] = ("psum", [128, 512], F32)
     PLACE["ps%d" % _k] = ("ps%d" % _k, 0, 512)
@@ -233,8 +235,8 @@ def rank_program(g, core, T, topo):
     def wrapped(sc, n, lo=0):
         return R(sc, lo + 15, n, 16)
 
-    def lifted(out, sc, lo, hi):
-        ts(out, wrapped(sc, hi, lo), R("up", 0, 1), Op.add)
+    def lifted(out, i, plus=0.0):
+        ts2(out, i, R("up", 0, 1), Op.add, plus, Op.add)
 
     def weave(chain, between, lead=False):
         between = list(between) + [None] * len(chain)
@@ -302,7 +304,7 @@ def rank_program(g, core, T, topo):
 
     def pads(name, tiles):
         for at, w, s in tiles:
-            lo = 16 * min(m for m in s if m != EQ) + 16 if len(s) == 4 else 0
+            lo = 16 * min(m for m in s if m >= 0) + 16 if len(s) == 4 else 0
             yield R(name, 4 * (at + lo), 4 * (at + w))
 
     EARLY = [tile for tile in OT if EQ not in tile[2] and max(tile[2]) < 16]
@@ -316,11 +318,11 @@ def rank_program(g, core, T, topo):
     choose(R("grp"), R("blk"), [[16, 8], [0, 16]], Op.is_ge, 15, -1)
     for r in pads("of", LATE[-1:] + EARLY + LATE[:-1]):
         fill(r, 0)
-    iota(R("io"), [[1, 768]], 0, 0)
+    iota(R("io"), [[1, 528]], -256, 0)
+    count = R("io", 256, 512)
     for r in pads("pf", PT):
         fill(r, 0)
-    fill(R("aux"), 0)
-    fill(R("pb1"), 1)
+    fill(R("pb1"), -512)
     iota(R("io2"), [[0, 2], [1, 256]], 0, 0)
     fill(R("at1"), 256)
 
@@ -336,7 +338,6 @@ def rank_program(g, core, T, topo):
     copy(R("ex0"), R("c16i", 0, 8))
     for b in range(4):
         copy(R("ct0", 512 * b + b, 512 * b + 512, 4), R("unit"))
-    zeros = R("ct0", 3, 1024, 4)
     memset(R("ors", 0, 1), 0.0)
     memset(R("prs", 0, 1), 0.0)
     quant("u", "ut")
@@ -347,9 +348,9 @@ def rank_program(g, core, T, topo):
     for t in range(4):
         act(R("ct1", t, 512, 4), R("grp"))
     act(R("sub"), R("su"), off=R("ex0"))
-    for t, k in ((0, 1.0), (1, 1.0), (2, 16.0), (3, 16.0)):
+    for t, k in ((0, 16.0), (1, 16.0), (2, 1.0), (3, 1.0)):
         act(R("ct1", 512 + t, 1024, 4), R("grp"), scale=k)
-    for t, k in ((0, 0.0), (1, 0.0), (2, 1.0), (3, 1.0)):
+    for t, k in ((0, 16.0), (1, 16.0), (2, 0.0), (3, 0.0)):
         act(R("ct1", 1024 + t, 1536, 4), R("grp"), scale=k)
 
     SC = {"o": "osc_", "p": "psc"}
@@ -360,13 +361,18 @@ def rank_program(g, core, T, topo):
     def compare(p, at, t, m, bank=0):
         f = p + "f"
         ts(R(f, 4 * at + t, 4 * (at + 16 * m + 16), 4), ps(bank, 16 * m + 16), scalar_of(p, m), Op.is_gt)
-        if m:
+        if m > SHORT[p]:
             act(R("junk", 512 * t, 512 * t + 16 * m), R(f, 4 * at + t, 4 * (at + 16 * m), 4), accum=R(p + "rs", m, m + 1))
 
-    def compare_scalar(p, steps):
+    def short_sums(p, where):
+        for m in range(SHORT[p], 0, -1):
+            i, o = R(p + "f", 4 * where[m][0] + where[m][1], 4 * (where[m][0] + 16 * m), 4), R(p + "rs", m, m + 1)
+            op("v", lambda: g.vector.tensor_reduce(ap(o), ap(i), AxisListType.X, Op.add), [i], [o])
+
+    def compare_scalar(p, steps, bank=1):
         f = p + "f"
         for k, (at, t, m) in enumerate(steps):
-            act(R("junk", 512 * k, 512 * k + 16 * m + 16), ps(1, 16 * m + 16), fn=Fn.Sign, scale=-1.0, bias=scalar_of(p, m))
+            act(R("junk", 512 * k, 512 * k + 16 * m + 16), ps(bank, 16 * m + 16), fn=Fn.Sign, scale=-1.0, bias=scalar_of(p, m))
         for k, (at, t, m) in enumerate(steps):
             j = 512 * k + 16 * m
             act(R(f, 4 * at + t, 4 * (at + 16 * m), 4), R("junk", 512 * k, j), fn=Fn.Relu, scale=-1.0, accum=R(p + "rs", m, m + 1))
@@ -414,13 +420,14 @@ def rank_program(g, core, T, topo):
         for tile in EARLY[:-1]:
             if m == min(tile[2]) - 1:
                 packed("o", tile)
-        if m == 2:
+        if m == LOADED - 3:
             mask("omk", 256, 512, R("ps0", 256, 512))
-        if m == 1:
+        if m == LOADED - 4:
             maxima("omk", "osc_", 256, 512)
+        if m == LOADED - 5:
+            compare_scalar("o", [where[k] + (k,) for k in AHEAD])
     quant("c", "ct1", 0, 128)
     packed("o", EARLY[-1])
-    compare_scalar("o", [where[m] + (m,) for m in AHEAD])
     for k, (at, w, s) in enumerate(LATE[:-1]):
         for i, m in enumerate(m for m in s if m not in AHEAD):
             if m == EQ:
@@ -437,17 +444,14 @@ def rank_program(g, core, T, topo):
         act(R("th", 512 * b, 512 * b + 512), ps(4 + b, 512), scale=0.5)
     act(R("osr"), ps(1, 512))
     act(R("cs"), R("dm"), fn=Fn.Identity, scale=2.0, bias=2 * FAR)
+    short_sums("o", where)
     quant("c", "ct1", 128, 256)
-    sort_end(512, "o", "rk", "rku", lambda: quant("v", "vt"), lambda: memset(R("ww"), 9e29), lambda: copy(R("rki"), R("rk")))
+    sort_end(512, "o", "rk", "rku", lambda: quant("v", "vt"), lambda: memset(R("ssc", 512, 528), 9e29), lambda: copy(R("rki"), R("rk")))
     scatter(R("lst"), R("rku"), R("io", 0, 512))
 
-    def pair_up(z, lst, offs, win, mid, *between):
+    def pair_up(z, offs, win, mid, *between):
         even, odd = R(offs, 0, 16), R(offs, 16, 32)
-        weave([lambda: wrap("lsc", 0, 256, R(lst, 0, 512, 2))], between[:1], lead=True)
-        wrap("lsc", 256, 512, R(lst, 1, 512, 2))
-        lifted(even, "lsc", 0, 256)
-        lifted(odd, "lsc", 256, 512)
-        copy(mid(3), win(3), off=even)
+        weave([lambda: copy(mid(3), win(3), off=even)], between[:1])
         for t in range(3):
             act(mid(t), win(t), off=even)
         for t in (3, 0, 1, 2):
@@ -455,85 +459,96 @@ def rank_program(g, core, T, topo):
         weave([lambda: quant(z, z)], between[1:], lead=True)
         send_mx(z, "l" + z, nxt, "r" + z)
 
-    pair_up("z1", "lst", "lu", lambda t: R("th", 512 * t, 512 * t + 512), lambda t: R("h", 768 * t, 768 * t + 512, 2),
-            lambda: ts(R("rkh"), R("rki"), 1, Op.arith_shift_right), lambda: copy(R("rhu"), R("rkh")))
+    ts(R("rkh"), R("rki"), 1, Op.arith_shift_right)
+    for c in range(2):
+        wrap("lsc", 256 * c, 256 * c + 256, R("lst", c, 512, 2))
+    lifted(R("lu"), wrapped("lsc", 512), 256.0)
+    pair_up("z1", "lu", lambda t: R("th", 512 * t, 512 * t + 512), lambda t: R("h", 768 * t, 768 * t + 512, 2),
+            lambda: ts2(R("rkm"), R("rk"), R("up", 0, 1), Op.subtract, 256.0, Op.add), lambda: copy(R("rhu"), R("rkh")))
 
     for c in range(2):
         act(R("ssr", c, 512, 2), R("osr"), off=R("lu", 16 * c, 16 * c + 16))
     wrap_sorted("ssc", 512, R("ssr"))
     wrap_sorted("pvs", 32, R("ssr", 15, 512, 16))
-    copy(R("ww", 0, 32), wrapped("ssc", 512))
-    fill(R("pb2"), 1)
-    iota(R("at2"), [[1, 768]], 0, 0)
+    fill(R("pb2"), -512)
+    fill(R("at2"), 768)
     for b in ("ra", "rb", "rc"):
         fill(R(b, 256, 272), 256)
     for b in ("d1q", "d0h"):
         for t in range(4):
             fill(R(b, 272 * t + 256, 272 * t + 272), 0)
 
-    def layer(q, tile, on_vector=(1, 3)):
+    def layer(q, tile, lo=0, n=256, bank=4, between=None):
         for b in range(4):
-            mm(4 + b, 256, "w", 128 * b, q)
+            mm(bank + b, n, "w", 128 * b, q, m0=lo)
         for b in range(4):
-            if b in on_vector:
-                ts(R(tile, b, 1024, 4), ps(4 + b, 256), 0.03125, Op.mult)
+            if b % 2:
+                ts(R(tile, 4 * lo + b, 4 * (lo + n), 4), ps(bank + b, n), 0.03125, Op.mult)
+                if b == 1 and between:
+                    between()
             else:
-                act(R(tile, b, 1024, 4), ps(4 + b, 256), scale=0.03125)
+                act(R(tile, 4 * lo + b, 4 * (lo + n), 4), ps(bank + b, n), scale=0.03125)
 
     def merge(t, need, sorted_, between):
         s = str(t)
-        layer("lz" + s, "pt")
-        quant("p" + s, "pt")
+        layer("lz" + s, "pt", 0, 128, 4)
+        layer("lz" + s, "pt", 128, 128, 0, lambda: quant("p" + s, "pt", 0, 128))
+        quant("p" + s, "pt", 128, 128)
+        mm(4, 128, "ub", 0, "p" + s)
+        mm(5, 128, "ub", 0, "p" + s)
         mm(0, 256, "ub", 0, "p" + s)
         mm(1, 256, "ub", 0, "p" + s)
-        steps = [(tile[0], k, m) for tile in PT for k, m in enumerate(tile[2])]
-        mine = iter(steps[SCALARS[t]:])
+        at = {m: (tile[0], k) for tile in PT for k, m in enumerate(tile[2])}
 
-        def step(n=1):
-            for _ in range(n):
-                compare("p", *next(mine))
+        def slot(m, lo=0, hi=256):
+            return R("pf", 4 * (at[m][0] + lo) + at[m][1], 4 * (at[m][0] + hi), 4)
 
-        def pivot(k):
-            ts(R("aux", 2 + k, 1024, 4), ps(0, 256), R("pvs", 16 * k + 15, 16 * k + 16), Op.is_ge)
-        mask("pmk", 0, 256, ps(0, 256))
-        pivot(0)
-        maxima("pmk", "psc", 0, 256)
-        if need > 256:
-            pivot(1)
-        else:
-            quant("seg", "aux")
+        def steps(hi, lo, bank=0):
+            for m in range(hi, lo - 1, -1):
+                compare("p", at[m][0], at[m][1], m, bank)
+
+        def begin(half, src, last):
+            lo, hi = 128 * half, 128 * half + 128
+            pivot = [lambda k=k: ts(slot(PIVOTS[k], lo, hi), src, R("pvs", 16 * k + 15, 16 * k + 16), Op.is_ge)
+                     for k in range(need // 256)]
+            weave([lambda: mask("pmk", lo, hi, src), lambda: maxima("pmk", "psc", lo, hi)], pivot + [last])
+        begin(0, ps(4, 128), None)
+        compare_scalar("p", [at[m] + (m,) for m in (7, 6)], 5)
+        steps(5, 5, 4)
+        steps(1, 0, 4)
         act(R("psr"), ps(1, 256))
-        compare_scalar("p", steps[:SCALARS[t]])
-        step()
-        if need > 256:
-            quant("seg", "aux")
-        mm(3, 256, "c", 256, "seg")
+        begin(1, R("ps0", 128, 256), None)
+        compare_scalar("p", [at[m] + (m,) for m in range(15, 15 - SCALARS[t], -1)])
+        steps(4, 4)
+        packed("p", PT[4])
+        mm(3, 256, "c", 256, "pf", m0=PT[4][0])
+        mm(2, 256, "c", 128, "pf", m0=PT[4][0], start=True, stop=False)
         for b in range(4):
             mm(4 + b, 256, "e", 128 * b, "p" + s)
-        step(7 - SCALARS[t])
-        equal(R("aux", 0, 1024, 4), 256, "p")
+        steps(15 - SCALARS[t], 8)
+        equal(slot(EQ), 256, "p")
         wrap("lsc", 0, 256, ps(3, 256))
-        packed("p", PT[1])
-        lifted(R("segu"), "lsc", 0, 256)
-        step()
-        tt(R("aux", 1, 1024, 4), R("ww"), R("psr"), Op.is_le, off=R("segu"))
-        step()
-        quant("aux", "aux")
-        mm(2, 256, "c", 128, "aux", start=True, stop=False)
-        added("p", PT[1])
-        step(3)
         summed("p", PT[2])
-        step(3)
+        lifted(R("segu"), wrapped("lsc", 256), 15.0)
+        steps(3, 2)
+        tt(slot(SEGMENT), R("ssc"), R("psr"), Op.is_le, off=R("segu"))
         summed("p", PT[0])
+        summed("p", PT[1])
         summed("p", PT[3], last=True)
+        short_sums("p", at)
         for b in range(4):
             act(R("h", 768 * b + 512, 768 * b + 768), ps(4 + b, 256), scale=0.5)
         sorted_()
         sort_end(256, "p", "pl" + s, "plu" + s)
-        pb, ob, pl = R("pb" + s), R("ob" + s), R("plu" + s)
-        weave([lambda: scatter(pb, pl, zeros),
-               lambda: scan(R("ob" + s, 0, need), R("pb" + s, 0, need), R("io", 0, need), -1.0, Op.add, Op.min),
-               lambda: scatter(ob, pl, R("io", 512, 768))], between, lead=True)
+        pb, k = "pb" + s, need // 256
+        weave([lambda: scatter(R(pb), R("plu" + s), count),
+               lambda: ts(R("fl", 0, need), R(pb, 0, need), 0.0, Op.is_lt)], between, lead=True)
+        for c in range(k):
+            wrap("lsc", 256 * c, 256 * c + 256, R(pb, c, need, k))
+        weave([lambda: scan(R("ob", 0, need), R("fl", 0, need), R("cs", 0, need), -513.0, Op.add, Op.min),
+               lambda: [wrap("sco", 256 * c, 256 * c + 256, R("ob", c, need, k)) for c in range(k)],
+               lambda: tt(R("lm", 0, need // 16), wrapped("lsc", need), wrapped("sco", need), Op.max),
+               lambda: lifted(R("elu" + s), R("lm", 0, need // 16), 512.0)], between[2:])
 
     held = lambda t: R("h", 768 * t, 768 * t + 768)
 
@@ -543,40 +558,40 @@ def rank_program(g, core, T, topo):
     merge(1, 512, odd_columns,
           [lambda: ts(R("pli"), R("pl1"), 512.0, Op.min), lambda: ts(R("plh"), R("pli"), 1, Op.arith_shift_right),
            lambda: copy(R("a1u"), R("plh"))])
-    pair_up("z2", "ob1", "elu1", held, lambda t: R("mid", 256 * t, 256 * t + 256))
+    pair_up("z2", "elu1", held, lambda t: R("mid", 256 * t, 256 * t + 256))
     send_list("a1u", [("la1", prv)], "ra1")
 
     scatter(R("at1"), R("elu1"), R("io2"))
-    fill(R("aux", 3, 1024, 4), 0)
+    fill(R("pf", 4 * PT[4][0] + 1, 4 * PF, 4), 0)
     for t in range(4):
-        act(R("wm", 768 * t, 768 * t + 512), R("h", 768 * t, 768 * t + 512), scale=2.0)
+        act(R("wm", 768 * t + 256, 768 * t + 768), R("h", 768 * t, 768 * t + 512), scale=2.0)
 
     def send_places():
         ts(R("a2u"), R("pl2"), 256.0, Op.min)
         send_list("a2u", [("la2n", prv), ("la2m", prv2)], "ra2")
-    merge(2, 256, lambda: act(R("gh"), R("at1"), off=R("rku")), [send_places, None, lambda: wrap("sch", 0, 512, R("gh"))])
-    lifted(R("h1u"), "sch", 0, 512)
-    wrap("lsc", 0, 256, R("ob2", 0, 256))
-    lifted(R("elu2"), "lsc", 0, 256)
-    act(R("rb", 0, 256), R("io", 0, 264), off=R("la2m"))
-    act(R("ra", 0, 256), R("io", 0, 264), off=R("la2n"))
-    act(R("rc", 0, 256), R("rb"), off=R("la1"))
+    merge(2, 256, lambda: act(R("gh"), R("at1"), off=R("rku")),
+          [send_places, None, lambda: wrap("sch", 0, 512, R("gh")), None, lambda: lifted(R("h1u"), wrapped("sch", 512))])
+    act(R("rb", 0, 256), R("io", 256, 528), off=R("la2m"))
+    act(R("ra", 0, 256), R("io", 256, 528), off=R("la2n"))
     for t in (1, 0, 3, 2):
         if t % 2:
             act(R("et", t, 1024, 4), held(t), scale=2.0, off=R("elu2"))
         else:
             ts(R("et", t, 1024, 4), held(t), 2.0, Op.mult, off=R("elu2"))
-    quant("et", "et")
     act(R("g1"), R("ra"), off=R("h1u"))
-    scatter(R("at2"), R("elu2"), R("io", 512, 768))
-    layer("et", "v2", (2, 3))
+    act(R("rc", 0, 256), R("rb"), off=R("la1"))
+    scatter(R("at2"), R("elu2", 0, 8), R("io", 256, 384))
+    quant("et", "et")
+    scatter(R("at2"), R("elu2", 8, 16), R("io", 384, 512))
+    wrap("sc1", 0, 512, R("g1"))
+    layer("et", "v2")
     act(R("g2"), R("at2"), off=R("rku"))
     quant("v2", "v2")
     send_mx("v2", "lv2", prv, "rv2")
     act(R("g0"), R("rc"), off=R("rhu"))
 
     def first_mean(t):
-        tt(R("wm", 768 * t + 512, 768 * t + 768), R("et", t, 1024, 4), R("v2", t, 1024, 4), Op.add)
+        tt(R("wm", 768 * t, 768 * t + 256), R("et", t, 1024, 4), R("v2", t, 1024, 4), Op.add)
 
     def pick(t):
         act(R("x2q", 512 * t, 512 * t + 512), R("wm", 768 * t, 768 * t + 768), scale=0.125, off=R("p2u"))
@@ -584,15 +599,13 @@ def rank_program(g, core, T, topo):
     def second_mean(t):
         tt(R("x1h", 512 * t, 512 * t + 512), R("d1q", 272 * t, 272 * t + 272), R("x2q", 512 * t, 512 * t + 512), Op.add, off=R("o1u"))
 
-    def used(out, sc, bound, o):
-        ts2(R(out), wrapped(sc, 512), R("up", 0, 1), Op.add, bound, o)
-    wrap("sc1", 0, 512, R("g1"))
-    wrap("sc2", 0, 512, R("g2"))
     first_mean(0)
-    lifted(R("p2u"), "sc2", 0, 512)
-    pick(0)
+    wrap("sc2", 0, 512, R("g2"))
+    tt(R("pm"), wrapped("sc2", 512), R("rkm"), Op.min)
+    lifted(R("p2u"), R("pm"))
     for t in range(1, 4):
         first_mean(t)
+    pick(0)
     for b in range(4):
         mm(4 + b, 256, "e", 128 * b, "lv2")
     for b in range(4):
@@ -600,11 +613,11 @@ def rank_program(g, core, T, topo):
             copy(R("d1", b, 1024, 4), ps(4 + b, 256))
         else:
             act(R("d1", b, 1024, 4), ps(4 + b, 256))
-    lifted(R("o1u"), "sc1", 0, 512)
-    used("u2", "sc2", 512.0, Op.is_ge)
-    used("u1", "sc1", 256.0, Op.is_lt)
+    wrap("sc0", 0, 512, R("g0"))
     quant("d1", "d1")
     send_mx("d1", "ld1", prv, "rd1")
+    lifted(R("o1u", 0, 64), wrapped("sc1", 1024))
+    ts2(R("u2", 0, 96), wrapped("sc2", 1536), R("up", 0, 1), Op.add, 256.0, Op.is_lt)
     for b in range(4):
         act(R("d1q", 272 * b, 272 * b + 256), ps(4 + b, 256), scale=0.25)
         if b < 3:
@@ -613,13 +626,8 @@ def rank_program(g, core, T, topo):
         mm(b, 256, "e", 128 * b, "ld1")
     for b in range(4):
         act(R("d0h", 272 * b, 272 * b + 256), ps(b, 256), scale=0.5)
-    for t in range(3):
-        second_mean(t)
-    tt(R("ucs"), R("u2"), R("u1"), Op.add)
-    wrap("sc0", 0, 512, R("g0"))
-    second_mean(3)
-    lifted(R("o0u"), "sc0", 0, 512)
-    used("u0", "sc0", 256.0, Op.is_lt)
+    weave([lambda t=t: second_mean(t) for t in range(4)],
+          [None, lambda: tt(R("ucs"), R("u2"), R("u1"), Op.add), lambda: tt(R("uct"), R("ucs"), R("u0"), Op.add)])
 
     def store_counts():
         op("v", lambda: g.vector.transpose(ap(R("ucr")), ap(R("uct"))), [R("uct")], [R("ucr")])
@@ -642,11 +650,10 @@ def rank_program(g, core, T, topo):
         dma("a", lambda: g.scalar.dma_start(T.y[:, lo:hi], T.yo[:, lo:hi]), [R("yo", lo, hi)], [], "sty")
     for t in range(4):
         last_mean(t, 0, CUT)
-    tt(R("uct"), R("ucs"), R("u0"), Op.add)
+    store_counts()
     store(0, 0, CUT)
     for t in range(4):
         last_mean(t, CUT, 512)
-    store_counts()
     store(1, CUT, 512)
 
     for s in SEMAPHORES:

from concourse.bass import DstId, RemoteDMATransfer
from concourse.mybir import dt, AluOpType as Op, ActivationFunctionType as Fn, AxisListType

F8, U8, BF, F32, I32, U16, F16 = "float8_e4m3fn_x4", "uint8", "bfloat16", "float32", "int32", "uint16", "float16"
FAR = 4e29
DROP = 1024.0
SCRATCH = {}
PLACE = {}


def _b(dtype, **kw):
    for k in kw:
        SCRATCH[k] = ("sbuf", [128, kw[k]], dtype)
        PLACE[k] = (k, 0, kw[k])


def _pack(buf, dtype, **kw):
    at = 0
    for k in kw:
        PLACE[k] = (buf, at, kw[k])
        at += kw[k]
    SCRATCH[buf] = ("sbuf", [128, at], dtype)


def _same(buf, **kw):
    for k in kw:
        PLACE[k] = (buf, 0, kw[k])


def _mx(**kw):
    for k in kw:
        _b(F8, **{"q" + k: kw[k]})
        _b(U8, **{"s" + k: kw[k]})


EQ, SEGMENT, PIVOTS = -1, -2, [-3, -4]
AHEAD = [28, 24, 20, 16]
SCALARS = {1: 3, 2: 3}
SHORT = {"o": 4, "p": 4}
LOADED = 14
CUT = 320


def tiles_of(slots, n):
    out, at = [], 0
    for k in range(0, len(slots), 4):
        s = slots[k:k + 4]
        w = max(128, n if min(s) < 0 else 16 * max(s) + 16)
        out.append((at, w, s))
        at += w
    return out, at


OT, OF = tiles_of([EQ] + list(range(31, -1, -1)), 512)
PT, PF = tiles_of([15, 14, 13, 12, EQ, SEGMENT] + list(range(11, 1, -1)) + PIVOTS + [1, 0], 256)
_b(BF, xt=2048, ut=512, vt=512, ct0=2048, ct1=1536, ones=128, unit=128, blk=128, grp=128,
   of=4 * OF, pf=4 * PF, junk=2048, at1=768, ra=272, rb=272, rc=272,
   th=2048, h=3072, wm=3072, mid=1024, z1=1024, z2=1024, pt=1024, et=1024, v2=1024, d1=1024,
   d1q=1088, d0h=1088, x2q=2048, x1h=2048, xo=2048, rst=512, cw=512, cs=512, pb1=768, pb2=768, fl=512,
   io=528, io2=512, lst=512, at2=768)
_pack("gathered", BF, gh=512, g2=512, g1=512, g0=512)
_b(F32, dm=512, dm16=16, cw16=16, osr=512, psr=256, qmk=512, osc_=512, psc=256,
   ssr=512, ssc=528, pvs=32, ucr=32, yo=512)
_pack("scans", F16, lsc=512, sch=512, sc2=512, sc1=512, sc0=512, ob=512, sco=512)
_same("qmk", omk=512, pmk=256)
_same("scans", osc2=512, psc2=256)
_pack("small", F32, c16=32, ors=32, orc=32, rk=32, prs=16, prc=16, pl1=16, pl2=16, u2=32, u1=32, u0=32, ucs=32, uct=32,
      cwa=16, cwb=16, up=8, lm=32, rkm=32, pm=32)
_b(I32, ii=32, jj=32, pj=32)
_pack("whole", I32, c16i=32, pli=16, plh=16, rki=32, rkh=32)
_b(U16, ex0=8, pju=32, a1u=16, a2u=16, la1=16, la2n=16, la2m=16)
_pack("offs", U16, rku=32, rhu=32, lu=32, segu=16, plu1=16, plu2=16, elu1=32, elu2=16, h1u=32, p2u=32, o1u=32, o0u=32)
_mx(x=512, u=128, ub=128, v=128, w=512, e=512, c=384,
    z1=256, z2=256, lz1=256, lz2=256, p1=256, p2=256, et=256, v2=256, lv2=256, d1=256, ld1=256, xo=512)
for _k, _d in (("q", F8), ("s", U8)):
    _pack(_k + "flags", _d, **{_k + "of": OF, _k + "pf": PF})
for _k in range(8):
    SCRATCH["ps%d" % _k] = ("psum", [128, 512], F32)
    PLACE["ps%d" % _k] = ("ps%d" % _k, 0, 512)
LOADS = ["lx0", "lx1", "ldu", "ldv", "lwc", "lws"]
ARRIVE = ["rz1", "rz2", "rv2", "rd1", "ra1", "ra2"]
SEMAPHORES = ["c_t", "c_v", "c_a", "c_g", "sty", "sto", "sent"] + LOADS + ARRIVE


def rank_program(g, core, T, topo):
    rank = T.rank_of(core)
    if rank is None:
        return
    cores = T.cores
    N = len(cores)
    nxt, prv, prv2 = cores[(rank + 1) % N], cores[(rank - 1) % N], cores[(rank - 2) % N]
    queue = {"t": g.tensor, "v": g.vector, "a": g.scalar, "g": g, "s": g.sync}
    total = {}
    clock = {q: {} for q in queue}
    hist = {}

    def clash(a, b):
        if a[0] >= b[1] or b[0] >= a[1]:
            return False
        if a[2] == b[2] and a[2] > 1 and (a[0] - b[0]) % a[2]:
            return False
        return True

    def needs(q, rd, wr, acc=False):
        need = {}
        for rs, w in ((rd, False), (wr, True)):
            for r in rs:
                psum = r[0][:2] == "ps" and r[0][2:].isdigit()
                for (ev, eq, reg, ew) in hist.get(r[0], ()):
                    if psum:
                        if eq == q and ((acc and q == "t") or not (w or ew)):
                            continue
                    elif not (w or ew) or not clash(r[1:], reg):
                        continue
                    sem, val, snap = ev
                    if need.get(sem, (0,))[0] < val:
                        need[sem] = (val, snap)
        return need

    def do_waits(q, need):
        have = clock[q]
        need = {s: v for s, v in need.items() if have.get(s, 0) < v[0]}
        for s in list(need):
            others = [o for o in need if o != s and need[o][1].get(s, 0) >= need[s][0]]
            if any(need[s][1].get(o, 0) < need[o][0] for o in others):
                del need[s]
        for s, (val, snap) in need.items():
            queue[q].wait_ge(T.sem[s], val)
            for k, v in snap.items():
                have[k] = max(have.get(k, 0), v)
            have[s] = max(have.get(s, 0), val)

    def record(q, ev, rd, wr):
        for rs, w in ((rd, False), (wr, True)):
            for r in rs:
                l = hist.setdefault(r[0], [])
                if w and r[3] == 1:
                    l[:] = [e for e in l if not (r[1] <= e[2][0] and e[2][1] <= r[2])]
                l.append((ev, q, r[1:], w))

    def op(q, fn, rd, wr, acc=False):
        do_waits(q, needs(q, rd, wr, acc))
        s = "c_" + q
        total[s] = total.get(s, 0) + 1
        fn().then_inc(T.sem[s], 1)
        snap = dict(clock[q])
        snap[s] = total[s]
        record(q, (s, total[s], snap), rd, wr)

    def dma(q, fn, rd, wr, sem):
        do_waits(q, needs(q, rd, wr))
        total[sem] = total.get(sem, 0) + 16
        fn().then_inc(T.sem[sem], 16)
        record(q, (sem, total[sem], dict(clock[q])), rd, wr)

    def width(name):
        return PLACE[name][2]

    def R(name, lo=0, hi=None, st=1):
        buf, at, n = PLACE[name]
        return (buf, at + lo, at + (n if hi is None else hi), st)

    def ap(r):
        return T[r[0]][:, r[1]:r[2]] if r[3] == 1 else T[r[0]][:, r[1]:r[2]:r[3]]

    def by(r, off):
        return ap(r).indirect(ap(off))

    def memset(out, c):
        op("v", lambda: g.vector.memset(ap(out), c), [], [out])

    def copy(out, i, off=None):
        op("v", lambda: g.vector.tensor_copy(ap(out), by(i, off) if off else ap(i)), [i] + ([off] if off else []), [out])

    def scatter(win, off, i):
        op("v", lambda: g.vector.tensor_copy(by(win, off), ap(i)), [i, off], [win])

    def tt(out, a, b, o, off=None):
        op("v", lambda: g.vector.tensor_tensor(ap(out), by(a, off) if off else ap(a), ap(b), o),
           [a, b] + ([off] if off else []), [out])

    def ts(out, a, s1, o, off=None):
        col = isinstance(s1, tuple)
        op("v", lambda: g.vector.tensor_scalar(ap(out), by(a, off) if off else ap(a), ap(s1) if col else s1, None, o),
           [a] + ([off] if off else []) + ([s1] if col else []), [out])

    def ts2(out, a, s1, o1, s2, o2):
        col = isinstance(s1, tuple)
        op("v", lambda: g.vector.tensor_scalar(ap(out), ap(a), ap(s1) if col else s1, s2, o1, o2),
           [a] + ([s1] if col else []), [out])

    def scan(out, a, b, init, o0, o1):
        op("v", lambda: g.vector.tensor_tensor_scan(ap(out), ap(a), ap(b), init, o0, o1), [a, b], [out])

    def act(out, i, scale=1.0, off=None, accum=None, fn=Fn.Copy, bias=None):
        col = isinstance(bias, tuple)

        def f():
            kw = {}
            if scale != 1.0:
                kw["scale"] = scale
            if bias is not None:
                kw["bias"] = ap(bias) if col else bias
            if accum:
                kw["accum_out"] = ap(accum)
            return g.scalar.activation(ap(out), by(i, off) if off else ap(i), fn, **kw)
        op("a", f, [i] + ([off] if off else []) + ([bias] if col else []), [out] + ([accum] if accum else []))

    def quant(name, tile, c0=0, n=None):
        n = width("q" + name) if n is None else n
        q, s, t = R("q" + name, c0, c0 + n), R("s" + name, c0, c0 + n), R(tile, 4 * c0, 4 * (c0 + n))
        op("v", lambda: g.vector.quantize_mx(ap(q), ap(s), ap(t)), [t], [q, s])

    def mm(bank, n, sta, c0, mov, m0=0, start=True, stop=True):
        o = R("ps%d" % bank, 0, n)
        a, b = R("q" + sta, c0, c0 + 128), R("s" + sta, c0, c0 + 128)
        c, d = R("q" + mov, m0, m0 + n), R("s" + mov, m0, m0 + n)
        op("t", lambda: g.tensor.matmul_mx(ap(o), ap(a), ap(b), ap(c), ap(d), start, stop), [a, b, c, d], [o], acc=not start)

    def ps(k, n):
        return R("ps%d" % k, 0, n)

    def mask(mk, lo, hi, src):
        tt(R(mk, lo, hi), src, R("dm", 0, hi - lo), Op.add)

    def maxima(mk, sc, lo, hi):
        scan(R(sc, lo, hi), R("rst", 0, hi - lo), R(mk, lo, hi), -FAR, Op.min, Op.max)

    def wrap_sorted(sc, n, src):
        scan(R(sc, 0, n), R("cs", 0, n), src, -FAR, Op.add, Op.min)

    def wrap(sc, lo, hi, src):
        scan(R(sc, lo, hi), R("cw", 0, hi - lo), src, 0.0, Op.add, Op.min)

    def wrapped(sc, n, lo=0):
        return R(sc, lo + 15, n, 16)

    def lifted(out, i, plus=0.0):
        ts2(out, i, R("up", 0, 1), Op.add, plus, Op.add)

    def weave(chain, between, lead=False):
        between = list(between) + [None] * len(chain)
        for f, o in zip(chain, between):
            for call in ((o, f) if lead else (f, o)):
                if call:
                    call()

    def engines(dst, a, b):
        m = 0
        for e in topo.engines(core, dst)[a:b]:
            m |= 1 << e
        return m

    def send_mx(src, land, dst, sem):
        rid, pid, _ = topo.addr(dst)
        ne = len(topo.engines(core, dst))
        q, s, lq, ls = R("q" + src), R("s" + src), R("q" + land), R("s" + land)
        do_waits("g", needs("g", [q, s], []))
        g.remote_dma(out_ap=ap(lq).bitcast(dt.uint8), in_ap=ap(q).bitcast(dt.uint8), remote_sem=T.sem[sem],
                     local_sem=T.sem.sent, pid=pid, routing_id=rid, dma_engine_mask=engines(dst, 0, ne))
        g.remote_dma(out_ap=ap(ls), in_ap=ap(s), remote_sem=T.sem[sem],
                     local_sem=T.sem.sent, pid=pid, routing_id=rid, dma_engine_mask=engines(dst, 0, ne))
        total["sent"] = total.get("sent", 0) + 2 * ne
        total[sem] = 2 * ne
        for r in (lq, ls):
            hist.setdefault(r[0], []).append(((sem, 2 * ne, {}), "r", r[1:], True))

    def send_list(src, pairs, sem):
        do_waits("g", needs("g", [R(src)], []))
        ids = []
        for land, dst in pairs:
            rid, pid, _ = topo.addr(dst)
            ids.append(DstId(rid=rid, pnc=pid))
        ne = min(len(topo.engines(core, dst)) for land, dst in pairs)
        g.remote_dma_fused([RemoteDMATransfer(dst_ids=ids, dma_engine_mask=engines(pairs[0][1], 0, ne), remote_sem=T.sem[sem],
                                              srcs=[T[src][:, :]], dsts=[T[land][:, :] for land, dst in pairs])],
                           local_sem=T.sem.sent)
        total["sent"] = total.get("sent", 0) + ne
        total[sem] = ne * len(pairs)
        for land, dst in pairs:
            hist.setdefault(land, []).append(((sem, total[sem], {}), "r", R(land)[1:], True))

    def load(q, out, src, sem, code=False):
        dma(q, lambda: queue[q].dma_start(ap(out).bitcast(dt.uint8) if code else ap(out), src), [], [out], sem)
    load("a", R("ut"), T.u[:, :], "ldu")
    load("s", R("xt", 0, 1024), T.x[:, 0:1024], "lx0")
    load("s", R("xt", 1024, 2048), T.x[:, 1024:2048], "lx1")
    do_waits("s", needs("s", [R("xt")], []))
    load("s", R("qw"), T.wc[:, :], "lwc", code=True)
    load("s", R("sw"), T.ws[:, :], "lws")
    load("s", R("vt"), T.v[:, :], "ldv")

    def iota(out, pattern, base, cm):
        if SCRATCH[out[0]][2] == I32:
            op("g", lambda: g.iota(ap(out), pattern, base, cm), [], [out])
        else:
            op("g", lambda: g.iota(ap(out), pattern, base, cm, allow_small_or_imprecise_dtypes=True), [], [out])

    def choose(out, i, pattern, cmp, base, cm):
        op("g", lambda: g.affine_select(ap(out), ap(i), pattern, cmp, 0.0, base, cm), [i], [out])

    def fill(out, c):
        iota(out, [[0, len(range(*out[1:]))]], c, 0)

    def pads(name, tiles):
        for at, w, s in tiles:
            lo = 16 * min(m for m in s if m >= 0) + 16 if len(s) == 4 else 0
            yield R(name, 4 * (at + lo), 4 * (at + w))

    EARLY = [tile for tile in OT if EQ not in tile[2] and max(tile[2]) < 16]
    LATE = [tile for tile in OT if tile not in EARLY]
    memset(R("ones"), 1.0)
    iota(R("ii"), [[1, 32]], 128, -1)
    iota(R("pj"), [[0, 32]], 0, 1)
    iota(R("c16i"), [[16, 32]], 0, 0)
    choose(R("unit"), R("ones"), [[-1, 128]], Op.is_equal, 0, 1)
    choose(R("blk"), R("ones"), [[-16, 8], [0, 16]], Op.is_ge, 0, 1)
    choose(R("grp"), R("blk"), [[16, 8], [0, 16]], Op.is_ge, 15, -1)
    for r in pads("of", LATE[-1:] + EARLY + LATE[:-1]):
        fill(r, 0)
    iota(R("io"), [[1, 528]], -256, 0)
    count = R("io", 256, 512)
    for r in pads("pf", PT):
        fill(r, 0)
    fill(R("pb1"), -512)
    iota(R("io2"), [[0, 2], [1, 256]], 0, 0)
    fill(R("at1"), 256)

    memset(R("ct0", 0, 1024), 0.0)
    ts(R("jj"), R("ii"), 15, Op.bitwise_and)
    memset(R("rst"), FAR)
    ts(R("ii"), R("pj"), 15, Op.bitwise_and)
    ts2(R("dm16"), R("jj", 0, 16), 0.0, Op.is_gt, -FAR, Op.mult)
    memset(R("rst", 0, 512, 16), -FAR)
    copy(R("pju"), R("ii"))
    act(R("dm"), R("dm16"), off=R("pju"))
    memset(R("ct0", 1024, 2048), 0.0)
    copy(R("ex0"), R("c16i", 0, 8))
    for b in range(4):
        copy(R("ct0", 512 * b + b, 512 * b + 512, 4), R("unit"))
    memset(R("ors", 0, 1), 0.0)
    memset(R("prs", 0, 1), 0.0)
    quant("u", "ut")
    ts2(R("cwa"), R("jj", 0, 16), 0.0, Op.is_equal, 2 * DROP, Op.mult)
    ts2(R("cwb"), R("jj", 0, 16), 1.0, Op.is_equal, -DROP, Op.mult)
    op("v", lambda: g.vector.tensor_copy(T.qub[:, 0:128].bitcast(dt.uint32), T.qu[:, 0:128].bitcast(dt.uint32).indirect(T.ex0[:, 0:8])),
       [R("qu"), R("ex0")], [R("qub")])
    for t in range(4):
        act(R("ct1", t, 512, 4), R("grp"))
    act(R("sub"), R("su"), off=R("ex0"))
    for t, k in ((0, 16.0), (1, 16.0), (2, 1.0), (3, 1.0)):
        act(R("ct1", 512 + t, 1024, 4), R("grp"), scale=k)
    for t, k in ((0, 16.0), (1, 16.0), (2, 0.0), (3, 0.0)):
        act(R("ct1", 1024 + t, 1536, 4), R("grp"), scale=k)

    SC = {"o": "osc_", "p": "psc"}

    def scalar_of(p, m):
        return R(SC[p], 16 * m + 15, 16 * m + 16)

    def compare(p, at, t, m, bank=0):
        f = p + "f"
        ts(R(f, 4 * at + t, 4 * (at + 16 * m + 16), 4), ps(bank, 16 * m + 16), scalar_of(p, m), Op.is_gt)
        if m > SHORT[p]:
            act(R("junk", 512 * t, 512 * t + 16 * m), R(f, 4 * at + t, 4 * (at + 16 * m), 4), accum=R(p + "rs", m, m + 1))

    def short_sums(p, where):
        for m in range(SHORT[p], 0, -1):
            i, o = R(p + "f", 4 * where[m][0] + where[m][1], 4 * (where[m][0] + 16 * m), 4), R(p + "rs", m, m + 1)
            op("v", lambda: g.vector.tensor_reduce(ap(o), ap(i), AxisListType.X, Op.add), [i], [o])

    def compare_scalar(p, steps, bank=1):
        f = p + "f"
        for k, (at, t, m) in enumerate(steps):
            act(R("junk", 512 * k, 512 * k + 16 * m + 16), ps(bank, 16 * m + 16), fn=Fn.Sign, scale=-1.0, bias=scalar_of(p, m))
        for k, (at, t, m) in enumerate(steps):
            j = 512 * k + 16 * m
            act(R(f, 4 * at + t, 4 * (at + 16 * m), 4), R("junk", 512 * k, j), fn=Fn.Relu, scale=-1.0, accum=R(p + "rs", m, m + 1))
            act(R(f, 4 * (at + 16 * m) + t, 4 * (at + 16 * m + 16), 4), R("junk", j, j + 16), fn=Fn.Relu, scale=-1.0)

    def equal(out, n, p):
        tt(out, R(SC[p], 0, n), ps(0, n), Op.is_equal)

    def packed(p, tile):
        quant(p + "f", p + "f", tile[0], tile[1])

    def added(p, tile, first=False, last=False):
        mm(2, tile[1], "c", 0, p + "f", m0=tile[0], start=first, stop=last)

    def summed(p, tile, first=False, last=False):
        packed(p, tile)
        added(p, tile, first, last)

    def sort_end(n, p, rk, u16, *between):
        weave([lambda: tt(R(p + "rc"), R("c16", 0, n // 16), R(p + "rs"), Op.subtract),
               lambda: wrap(p + "sc2", 0, n, ps(2, n)),
               lambda: tt(R(rk), wrapped(p + "sc2", n), R(p + "rc"), Op.add),
               lambda: copy(R(u16), R(rk))], (None,) + between)

    where = {m: (tile[0], t) for tile in OT for t, m in enumerate(tile[2])}
    quant("x", "xt", 0, 256)
    mm(3, 256, "ub", 0, "x")
    quant("e", "ct0", 0, 256)
    ts2(R("up", 0, 1), R("ii", 0, 1), 15.0, Op.is_lt, DROP, Op.mult)
    tt(R("cw16"), R("cwa"), R("cwb"), Op.add)
    ts2(R("c16"), R("c16i"), R("up", 0, 1), Op.add, -1.0, Op.add)
    act(R("cw"), R("cw16"), off=R("pju"))
    mask("omk", 0, 256, ps(3, 256))
    quant("e", "ct0", 256, 128)
    maxima("omk", "osc_", 0, 256)
    quant("e", "ct0", 384, 128)
    for m in range(15, -1, -1):
        compare("o", where[m][0], where[m][1], m, bank=3)
        if m == LOADED:
            quant("x", "xt", 256, 256)
            mm(0, 512, "ub", 0, "x")
            mm(1, 512, "ub", 0, "x")
            for b in range(4):
                mm(4 + b, 512, "e", 128 * b, "x")
        for tile in EARLY[:-1]:
            if m == min(tile[2]) - 1:
                packed("o", tile)
        if m == LOADED - 3:
            mask("omk", 256, 512, R("ps0", 256, 512))
        if m == LOADED - 4:
            maxima("omk", "osc_", 256, 512)
        if m == LOADED - 5:
            compare_scalar("o", [where[k] + (k,) for k in AHEAD])
    quant("c", "ct1", 0, 128)
    packed("o", EARLY[-1])
    for k, (at, w, s) in enumerate(LATE[:-1]):
        for i, m in enumerate(m for m in s if m not in AHEAD):
            if m == EQ:
                equal(R("of", 4 * at + s.index(EQ), 4 * (at + 512), 4), 512, "o")
            else:
                compare("o", at, where[m][1], m)
            if i == 0 and k > 0:
                summed("o", LATE[k - 1], first=k == 1)
                for early in EARLY if k == 1 else ():
                    added("o", early)
    summed("o", LATE[-1])
    summed("o", LATE[-2], last=True)
    for b in range(4):
        act(R("th", 512 * b, 512 * b + 512), ps(4 + b, 512), scale=0.5)
    act(R("osr"), ps(1, 512))
    act(R("cs"), R("dm"), fn=Fn.Identity, scale=2.0, bias=2 * FAR)
    short_sums("o", where)
    quant("c", "ct1", 128, 256)
    sort_end(512, "o", "rk", "rku", lambda: quant("v", "vt"), lambda: memset(R("ssc", 512, 528), 9e29), lambda: copy(R("rki"), R("rk")))
    scatter(R("lst"), R("rku"), R("io", 0, 512))

    def pair_up(z, offs, win, mid, *between):
        even, odd = R(offs, 0, 16), R(offs, 16, 32)
        weave([lambda: copy(mid(3), win(3), off=even)], between[:1])
        for t in range(3):
            act(mid(t), win(t), off=even)
        for t in (3, 0, 1, 2):
            tt(R(z, t, 1024, 4), win(t), mid(t), Op.add, off=odd)
        weave([lambda: quant(z, z)], between[1:], lead=True)
        send_mx(z, "l" + z, nxt, "r" + z)

    ts(R("rkh"), R("rki"), 1, Op.arith_shift_right)
    for c in range(2):
        wrap("lsc", 256 * c, 256 * c + 256, R("lst", c, 512, 2))
    lifted(R("lu"), wrapped("lsc", 512), 256.0)
    pair_up("z1", "lu", lambda t: R("th", 512 * t, 512 * t + 512), lambda t: R("h", 768 * t, 768 * t + 512, 2),
            lambda: ts2(R("rkm"), R("rk"), R("up", 0, 1), Op.subtract, 256.0, Op.add), lambda: copy(R("rhu"), R("rkh")))

    for c in range(2):
        act(R("ssr", c, 512, 2), R("osr"), off=R("lu", 16 * c, 16 * c + 16))
    wrap_sorted("ssc", 512, R("ssr"))
    wrap_sorted("pvs", 32, R("ssr", 15, 512, 16))
    fill(R("pb2"), -512)
    fill(R("at2"), 768)
    for b in ("ra", "rb", "rc"):
        fill(R(b, 256, 272), 256)
    for b in ("d1q", "d0h"):
        for t in range(4):
            fill(R(b, 272 * t + 256, 272 * t + 272), 0)

    def layer(q, tile, lo=0, n=256, bank=4, between=None):
        for b in range(4):
            mm(bank + b, n, "w", 128 * b, q, m0=lo)
        for b in range(4):
            if b % 2:
                ts(R(tile, 4 * lo + b, 4 * (lo + n), 4), ps(bank + b, n), 0.03125, Op.mult)
                if b == 1 and between:
                    between()
            else:
                act(R(tile, 4 * lo + b, 4 * (lo + n), 4), ps(bank + b, n), scale=0.03125)

    def merge(t, need, sorted_, between):
        s = str(t)
        layer("lz" + s, "pt", 0, 128, 4)
        layer("lz" + s, "pt", 128, 128, 0, lambda: quant("p" + s, "pt", 0, 128))
        quant("p" + s, "pt", 128, 128)
        mm(4, 128, "ub", 0, "p" + s)
        mm(5, 128, "ub", 0, "p" + s)
        mm(0, 256, "ub", 0, "p" + s)
        mm(1, 256, "ub", 0, "p" + s)
        at = {m: (tile[0], k) for tile in PT for k, m in enumerate(tile[2])}

        def slot(m, lo=0, hi=256):
            return R("pf", 4 * (at[m][0] + lo) + at[m][1], 4 * (at[m][0] + hi), 4)

        def steps(hi, lo, bank=0):
            for m in range(hi, lo - 1, -1):
                compare("p", at[m][0], at[m][1], m, bank)

        def begin(half, src, last):
            lo, hi = 128 * half, 128 * half + 128
            pivot = [lambda k=k: ts(slot(PIVOTS[k], lo, hi), src, R("pvs", 16 * k + 15, 16 * k + 16), Op.is_ge)
                     for k in range(need // 256)]
            weave([lambda: mask("pmk", lo, hi, src), lambda: maxima("pmk", "psc", lo, hi)], pivot + [last])
        begin(0, ps(4, 128), None)
        compare_scalar("p", [at[m] + (m,) for m in (7, 6)], 5)
        steps(5, 5, 4)
        steps(1, 0, 4)
        act(R("psr"), ps(1, 256))
        begin(1, R("ps0", 128, 256), None)
        compare_scalar("p", [at[m] + (m,) for m in range(15, 15 - SCALARS[t], -1)])
        steps(4, 4)
        packed("p", PT[4])
        mm(3, 256, "c", 256, "pf", m0=PT[4][0])
        mm(2, 256, "c", 128, "pf", m0=PT[4][0], start=True, stop=False)
        for b in range(4):
            mm(4 + b, 256, "e", 128 * b, "p" + s)
        steps(15 - SCALARS[t], 8)
        equal(slot(EQ), 256, "p")
        wrap("lsc", 0, 256, ps(3, 256))
        summed("p", PT[2])
        lifted(R("segu"), wrapped("lsc", 256), 15.0)
        steps(3, 2)
        tt(slot(SEGMENT), R("ssc"), R("psr"), Op.is_le, off=R("segu"))
        summed("p", PT[0])
        summed("p", PT[1])
        summed("p", PT[3], last=True)
        short_sums("p", at)
        for b in range(4):
            act(R("h", 768 * b + 512, 768 * b + 768), ps(4 + b, 256), scale=0.5)
        sorted_()
        sort_end(256, "p", "pl" + s, "plu" + s)
        pb, k = "pb" + s, need // 256
        weave([lambda: scatter(R(pb), R("plu" + s), count),
               lambda: ts(R("fl", 0, need), R(pb, 0, need), 0.0, Op.is_lt)], between, lead=True)
        for c in range(k):
            wrap("lsc", 256 * c, 256 * c + 256, R(pb, c, need, k))
        weave([lambda: scan(R("ob", 0, need), R("fl", 0, need), R("cs", 0, need), -513.0, Op.add, Op.min),
               lambda: [wrap("sco", 256 * c, 256 * c + 256, R("ob", c, need, k)) for c in range(k)],
               lambda: tt(R("lm", 0, need // 16), wrapped("lsc", need), wrapped("sco", need), Op.max),
               lambda: lifted(R("elu" + s), R("lm", 0, need // 16), 512.0)], between[2:])

    held = lambda t: R("h", 768 * t, 768 * t + 768)

    def odd_columns():
        for t in range(4):
            act(R("h", 768 * t + 1, 768 * t + 512, 2), R("th", 512 * t, 512 * t + 512), off=R("lu", 16, 32))
    merge(1, 512, odd_columns,
          [lambda: ts(R("pli"), R("pl1"), 512.0, Op.min), lambda: ts(R("plh"), R("pli"), 1, Op.arith_shift_right),
           lambda: copy(R("a1u"), R("plh"))])
    pair_up("z2", "elu1", held, lambda t: R("mid", 256 * t, 256 * t + 256))
    send_list("a1u", [("la1", prv)], "ra1")

    scatter(R("at1"), R("elu1"), R("io2"))
    fill(R("pf", 4 * PT[4][0] + 1, 4 * PF, 4), 0)
    for t in range(4):
        act(R("wm", 768 * t + 256, 768 * t + 768), R("h", 768 * t, 768 * t + 512), scale=2.0)

    def send_places():
        ts(R("a2u"), R("pl2"), 256.0, Op.min)
        send_list("a2u", [("la2n", prv), ("la2m", prv2)], "ra2")
    merge(2, 256, lambda: act(R("gh"), R("at1"), off=R("rku")),
          [send_places, None, lambda: wrap("sch", 0, 512, R("gh")), None, lambda: lifted(R("h1u"), wrapped("sch", 512))])
    act(R("rb", 0, 256), R("io", 256, 528), off=R("la2m"))
    act(R("ra", 0, 256), R("io", 256, 528), off=R("la2n"))
    for t in (1, 0, 3, 2):
        if t % 2:
            act(R("et", t, 1024, 4), held(t), scale=2.0, off=R("elu2"))
        else:
            ts(R("et", t, 1024, 4), held(t), 2.0, Op.mult, off=R("elu2"))
    act(R("g1"), R("ra"), off=R("h1u"))
    act(R("rc", 0, 256), R("rb"), off=R("la1"))
    scatter(R("at2"), R("elu2", 0, 8), R("io", 256, 384))
    quant("et", "et")
    scatter(R("at2"), R("elu2", 8, 16), R("io", 384, 512))
    wrap("sc1", 0, 512, R("g1"))
    layer("et", "v2")
    act(R("g2"), R("at2"), off=R("rku"))
    quant("v2", "v2")
    send_mx("v2", "lv2", prv, "rv2")
    act(R("g0"), R("rc"), off=R("rhu"))

    def first_mean(t):
        tt(R("wm", 768 * t, 768 * t + 256), R("et", t, 1024, 4), R("v2", t, 1024, 4), Op.add)

    def pick(t):
        act(R("x2q", 512 * t, 512 * t + 512), R("wm", 768 * t, 768 * t + 768), scale=0.125, off=R("p2u"))

    def second_mean(t):
        tt(R("x1h", 512 * t, 512 * t + 512), R("d1q", 272 * t, 272 * t + 272), R("x2q", 512 * t, 512 * t + 512), Op.add, off=R("o1u"))

    first_mean(0)
    wrap("sc2", 0, 512, R("g2"))
    tt(R("pm"), wrapped("sc2", 512), R("rkm"), Op.min)
    lifted(R("p2u"), R("pm"))
    for t in range(1, 4):
        first_mean(t)
    pick(0)
    for b in range(4):
        mm(4 + b, 256, "e", 128 * b, "lv2")
    for b in range(4):
        if b >= 2:
            copy(R("d1", b, 1024, 4), ps(4 + b, 256))
        else:
            act(R("d1", b, 1024, 4), ps(4 + b, 256))
    wrap("sc0", 0, 512, R("g0"))
    quant("d1", "d1")
    send_mx("d1", "ld1", prv, "rd1")
    lifted(R("o1u", 0, 64), wrapped("sc1", 1024))
    ts2(R("u2", 0, 96), wrapped("sc2", 1536), R("up", 0, 1), Op.add, 256.0, Op.is_lt)
    for b in range(4):
        act(R("d1q", 272 * b, 272 * b + 256), ps(4 + b, 256), scale=0.25)
        if b < 3:
            pick(b + 1)
    for b in range(4):
        mm(b, 256, "e", 128 * b, "ld1")
    for b in range(4):
        act(R("d0h", 272 * b, 272 * b + 256), ps(b, 256), scale=0.5)
    weave([lambda t=t: second_mean(t) for t in range(4)],
          [None, lambda: tt(R("ucs"), R("u2"), R("u1"), Op.add), lambda: tt(R("uct"), R("ucs"), R("u0"), Op.add)])

    def store_counts():
        op("v", lambda: g.vector.transpose(ap(R("ucr")), ap(R("uct"))), [R("uct")], [R("ucr")])
        for k in range(2):
            dma("s", lambda: g.sync.dma_start(T.uc[k:8:2, :], T.ucr[:, 16 * k:16 * k + 16]), [R("ucr")], [], "sto")

    def last_mean(t, lo, hi):
        tt(R("xo", 4 * lo + t, 4 * hi, 4), R("d0h", 272 * t, 272 * t + 272), R("x1h", 512 * t + lo, 512 * t + hi), Op.add,
           off=R("o0u", lo // 16, hi // 16))

    def store(c, lo, hi):
        quant("xo", "xo", lo, hi - lo)
        q = R("qxo", lo, hi)
        dma("s", lambda: g.sync.dma_start(T.oc[:, 4 * lo:4 * hi], ap(q).bitcast(dt.uint8)), [q], [], "sto")
        mm(4 + c, hi - lo, "v", 0, "xo", m0=lo)
        for k in range(4):
            e, o, i = ("s", "a")[k // 2], T.osc[4 * k:4 * k + 4, lo:hi], T.sxo[32 * k:32 * k + 4, lo:hi]
            dma(e, lambda: queue[e].dma_start(o, i), [R("sxo", lo, hi)], [], "sto" if e == "s" else "sty")
        act(R("yo", lo, hi), ps(4 + c, hi - lo))
        dma("a", lambda: g.scalar.dma_start(T.y[:, lo:hi], T.yo[:, lo:hi]), [R("yo", lo, hi)], [], "sty")
    for t in range(4):
        last_mean(t, 0, CUT)
    store_counts()
    store(0, 0, CUT)
    for t in range(4):
        last_mean(t, CUT, 512)
    store(1, CUT, 512)

    for s in SEMAPHORES:
        if total.get(s, 0):
            g.wait_ge(T.sem[s], total[s])
